import numpy as np
import ml_dtypes


def mxq(x, axis, fmt="e4m3"):
    dtype, down = {"e4m3": (ml_dtypes.float8_e4m3fn, 7), "e5m2": (ml_dtypes.float8_e5m2, 14)}[fmt]
    v = np.moveaxis(np.asarray(x, np.float32).astype(ml_dtypes.bfloat16).astype(np.float64), axis, -1)
    blocks = v.reshape(v.shape[:-1] + (-1, 32))
    amax = np.abs(blocks).max(-1, keepdims=True)
    byte = np.maximum(np.where(amax > 0, np.frexp(amax)[1] - 1 + 127, 0) - down, 1)
    scale = np.exp2(byte - 127.0)
    codes = (blocks / scale).astype(np.float32).astype(dtype).astype(np.float64)
    return np.moveaxis((codes * scale).reshape(v.shape), -1, axis)


WIDE = False


def mx_kscale(k):
    if not WIDE:
        return np.ones(k)
    levels = np.array([10, -10, 5, -5, 0])
    if k % 512:
        return np.exp2(np.random.permutation(np.resize(levels, k // 32))).repeat(32)
    a = np.empty((k // 512, 16))
    for p in range(k // 512):
        a[p, :8] = np.random.permutation(np.resize(levels, 8))
        for g in range(8):
            far = levels[np.abs(levels - a[p, g]) >= 10]
            a[p, g + 8] = far[np.random.randint(len(far))]
    return np.exp2(a.ravel()).repeat(32)


def f64(x):
    return np.asarray(x).astype(np.float64)


def striped(idx):
    return np.tile(np.asarray(idx).reshape(-1, 16).T, (8, 1)).astype(np.uint16)


def unstriped(offs):
    return offs[:16].T.reshape(-1).astype(np.int64)


E2M1 = np.array([0.0, 0.5, 1.0, 1.5, 2.0, 3.0, 4.0, 6.0, -0.0, -0.5, -1.0, -1.5, -2.0, -3.0, -4.0, -6.0])


def pack_weight(w, fmt):
    k, n = w.shape
    w = f64(np.asarray(w, np.float32).astype(ml_dtypes.bfloat16)).reshape(k // 32, 32, n)
    amax = np.abs(w).max(1)
    if fmt == "e4m3":
        byte = np.frexp(amax)[1] - 1 + 127 - 7
    else:
        mant, ex = np.frexp(amax / 6.0)
        byte = np.where(mant > 0.5, ex, ex - 1) + 127
    byte = np.clip(np.where(amax > 0, byte, 1), 1, 254)
    scaled = (w * np.exp2(127.0 - byte)[:, None, :]).reshape(k, n).astype(np.float32)
    by_word = np.ascontiguousarray(scaled.reshape(k // 512, 128, 4, n).transpose(0, 1, 3, 2))
    if fmt == "e4m3":
        words = by_word.astype(ml_dtypes.float8_e4m3fn).view(np.uint8)
    else:
        c = by_word.astype(ml_dtypes.float4_e2m1fn).view(np.uint8) & 0xF
        words = (c[..., 0::2] | (c[..., 1::2] << 4)).reshape(k // 512, 128, 2 * n)
    return np.ascontiguousarray(words), np.ascontiguousarray(byte.astype(np.uint8).reshape(k // 512, 16, n))


def unpack_weight(words, scales, fmt):
    g, _, n = scales.shape
    words = np.ascontiguousarray(words).reshape(g, 128, n, -1)
    if fmt == "e4m3":
        vals = words.view(ml_dtypes.float8_e4m3fn).astype(np.float64)
    else:
        nib = np.empty((g, 128, n, 4), np.uint8)
        nib[..., 0::2] = words & 0xF
        nib[..., 1::2] = words >> 4
        vals = E2M1[nib]
    vals = vals * np.repeat(np.exp2(scales.astype(np.float64) - 127.0), 8, axis=1)[..., None]
    return vals.transpose(0, 1, 3, 2).reshape(g * 512, n)


B, N, T, D, NQ = 1, 512, 2048, 512, 512
SEG = 16


def setup_inputs():
    n = np.random.standard_normal
    idx = np.random.permutation(T)[:B * N]
    s = mx_kscale(D)[:, None]
    kp = pack_weight(n((D, T)) / s, "e4m3")
    return {
        "qT": (n((B, D, NQ)) * s * (1.00 / np.sqrt(D))).astype(np.float32),
        "k_words": kp[0],
        "k_scales": kp[1],
        "hw": (np.random.uniform(-0.5, 1.0, (B, 1, NQ))).astype(np.float32),
        "offs": striped(idx),
    }


def reference(qT, k_words, k_scales, hw, offs):
    idx = unstriped(offs)
    pick = lambda x, which: x[:, which].reshape(x.shape[0], B, -1).transpose(1, 0, 2)
    k = unpack_weight(k_words, k_scales, "e4m3")
    kg = pick(k, idx)
    qq = mxq(f64(qT), 1, "e4m3")
    a = kg.transpose(0, 2, 1) @ qq
    y = (np.maximum(a, 0.0) * f64(hw)).reshape(B, N, NQ // SEG, SEG).sum(-1)
    return y

@@ -1,0 +1,139 @@
+from contextlib import ExitStack
+
+import concourse.mybir as mybir
+from concourse.masks import make_identity
+
+F32 = mybir.dt.float32
+BF16 = mybir.dt.bfloat16
+I32 = mybir.dt.int32
+U32 = mybir.dt.uint32
+U16 = mybir.dt.uint16
+U8 = mybir.dt.uint8
+FP8X4 = mybir.dt.float8_e4m3fn_x4
+ALU = mybir.AluOpType
+AX = mybir.AxisListType
+
+P = 128
+PACK = 4
+N, T, D, NQ, SEG = 512, 2048, 512, 512, 16
+TILES = N // P
+FLOPS = 2 * N * D * NQ
+
+
+def tile_attend_indexer_topk_kernel(tc, qT, k_words, k_scales, hw, offs, out):
+    nc = tc.nc
+    with ExitStack() as ctx:
+        sb = ctx.enter_context(tc.tile_pool(name="sb", bufs=1))
+        ps = ctx.enter_context(tc.psum_pool(name="ps", bufs=1))
+
+        offsets = sb.tile([P, N // 16], U16, name="offsets")
+        pool_words = sb.tile([P, T], I32, name="pool_words", align_bytes=64)
+        pool_scales = sb.tile([P, T], U8, name="pool_scales", align_bytes=64)
+        key_words = sb.tile([P, N], U32, name="key_words", align_bytes=64)
+        key_scales = sb.tile([P, N], U8, name="key_scales", align_bytes=64)
+        hw_cols = sb.tile([P, PACK], F32, name="hw_cols")
+        hw_rows = sb.tile([P, NQ], F32, name="hw_rows")
+        ident = sb.tile([P, P], F32, name="ident")
+        result = sb.tile([P, TILES, NQ // SEG], F32, name="result")
+        q_words = sb.tile([P, NQ], U32, name="q_words", align_bytes=64)
+        q_scales = sb.tile([P, NQ], U8, name="q_scales", align_bytes=64)
+
+        loads = [(0, 128), (128, 256), (256, 512)]
+        raw = [sb.tile([P, PACK, b - a], F32, name="raw%d" % a) for a, b in loads]
+        q_rows = qT[0].rearrange("(p t) q -> p t q", t=PACK)
+
+        nc.vector.memset(pool_scales[:].bitcast(I32), 0)
+        nc.sync.dma_start(offsets[:], offs)
+        nc.sync.dma_start(hw_cols[:], hw[0].rearrange("o (p c) -> p (o c)", c=PACK))
+        nc.sync.dma_start(raw[0][:], q_rows[:, :, 0:128])
+        scale_rows = k_scales[0].bitcast(I32)
+        for quad in range(4):
+            nc.sync.dma_start(
+                pool_scales[32 * quad : 32 * quad + 4, :].bitcast(I32), scale_rows[4 * quad : 4 * quad + 4, :]
+            )
+        nc.sync.dma_start(pool_words[:], k_words[0].rearrange("p n t -> p (n t)").bitcast(I32))
+        nc.sync.dma_start(raw[1][:], q_rows[:, :, 128:256])
+        nc.sync.dma_start(raw[2][:], q_rows[:, :, 256:512])
+
+        make_identity(nc, ident[:])
+        hw_ps = ps.tile([P, PACK, P], F32, name="hw_ps")
+        for c in range(PACK):
+            nc.tensor.transpose(hw_ps[:, c, :], hw_cols[:, c : c + 1].to_broadcast([P, P]), ident[:])
+
+        def interleave(src, a, b):
+            grouped = sb.tile([P, b - a, PACK], BF16, name="grouped%d" % a, align_bytes=64)
+            nc.scalar.copy(out=grouped[:], in_=src.rearrange("p t q -> p q t"))
+            return grouped
+
+        def quantize(grouped, a, b):
+            nc.vector.quantize_mx(
+                out=q_words[:, a:b].bitcast(FP8X4),
+                scales=q_scales[:, a:b],
+                in_=grouped[:].rearrange("p q t -> p (q t)"),
+            )
+
+        def scores(name, tiles, a, b):
+            acc = ps.tile([P, len(tiles), b - a], F32, name=name)
+            for n, s in enumerate(tiles):
+                nc.tensor.matmul_mx(
+                    out=acc[:, n, :],
+                    lhsT=key_words[:, s * P : (s + 1) * P].bitcast(FP8X4),
+                    lhsT_scale=key_scales[:, s * P : (s + 1) * P],
+                    rhs=q_words[:, a:b].bitcast(FP8X4),
+                    rhs_scale=q_scales[:, a:b],
+                    start=True,
+                    stop=True,
+                )
+            return acc
+
+        def weigh(name, acc, tiles, a, b):
+            shape = [P, len(tiles), b - a]
+            prod = sb.tile(shape, F32, name=name)
+            nc.vector.scalar_tensor_tensor(
+                out=prod[:],
+                in0=acc[:],
+                scalar=0.0,
+                in1=hw_rows[:, a:b].unsqueeze(1).to_broadcast(shape),
+                op0=ALU.max,
+                op1=ALU.mult,
+            )
+            return prod
+
+        def add_heads(prod, tiles, a, b):
+            nc.vector.tensor_reduce(
+                out=result[:, tiles[0] : tiles[-1] + 1, a // SEG : b // SEG],
+                in_=prod[:].rearrange("p s (j h) -> p s j h", h=SEG),
+                axis=AX.X,
+                op=ALU.add,
+            )
+
+        g0 = interleave(raw[0][:], 0, 128)
+        nc.scalar.copy(out=hw_rows[:].rearrange("m (p c) -> m p c", c=PACK), in_=hw_ps[:].rearrange("m c p -> m p c"))
+        nc.vector.tensor_copy(key_scales[:], pool_scales[:].indirect(offsets[:]))
+        quantize(g0, 0, 128)
+        g1 = interleave(raw[1][:], 128, 256)
+        g2 = interleave(raw[2][:], 256, 512)
+        window = pool_words[:].bitcast(U32)
+        half = N // 2
+        nc.vector.tensor_copy(key_words[:, :half], window.indirect(offsets[:, : half // 16]))
+        acc0a = scores("acc0a", [0, 1], 0, 128)
+        nc.vector.tensor_copy(key_words[:, half:], window.indirect(offsets[:, half // 16 :]))
+        acc0b = scores("acc0b", [2, 3], 0, 128)
+        p0a = weigh("p0a", acc0a, [0, 1], 0, 128)
+        quantize(g1, 128, 256)
+        acc1 = scores("acc1", [0, 1, 2, 3], 128, 256)
+        p0b = weigh("p0b", acc0b, [2, 3], 0, 128)
+        add_heads(p0a, [0, 1], 0, 128)
+        add_heads(p0b, [2, 3], 0, 128)
+        p1 = weigh("p1", acc1, [0, 1, 2, 3], 128, 256)
+        quantize(g2, 256, 512)
+        acc2 = scores("acc2", [0, 1], 256, 512)
+        acc3 = scores("acc3", [2, 3], 256, 512)
+        add_heads(p1, [0, 1, 2, 3], 128, 256)
+        p2 = weigh("p2", acc2, [0, 1], 256, 512)
+        p3 = weigh("p3", acc3, [2, 3], 256, 512)
+        rows = out[0].rearrange("(s p) j -> p s j", p=P)
+        add_heads(p2, [0, 1], 256, 512)
+        nc.sync.dma_start(rows[:, 0:2, :], result[:, 0:2, :])
+        add_heads(p3, [2, 3], 256, 512)
+        nc.sync.dma_start(rows[:, 2:4, :], result[:, 2:4, :])

@@ -12,11 +12,14 @@ U8 = mybir.dt.uint8
 FP8X4 = mybir.dt.float8_e4m3fn_x4
 ALU = mybir.AluOpType
 AX = mybir.AxisListType
+ACT = mybir.ActivationFunctionType
 
 P = 128
 PACK = 4
 N, T, D, NQ, SEG = 512, 2048, 512, 512, 16
-TILES = N // P
+GROUPS = NQ // P
+HALF = N // 2
+SCALAR_ROWS = 80
 FLOPS = 2 * N * D * NQ
 
 
@@ -31,109 +34,93 @@ def tile_attend_indexer_topk_kernel(tc, qT, k_words, k_scales, hw, offs, out):
         pool_scales = sb.tile([P, T], U8, name="pool_scales", align_bytes=64)
         key_words = sb.tile([P, N], U32, name="key_words", align_bytes=64)
         key_scales = sb.tile([P, N], U8, name="key_scales", align_bytes=64)
-        hw_cols = sb.tile([P, PACK], F32, name="hw_cols")
-        hw_rows = sb.tile([P, NQ], F32, name="hw_rows")
+        weights = sb.tile([P, GROUPS], F32, name="weights")
         ident = sb.tile([P, P], F32, name="ident")
-        result = sb.tile([P, TILES, NQ // SEG], F32, name="result")
+        raw = sb.tile([P, PACK, NQ], F32, name="raw")
+        grouped = sb.tile([P, GROUPS, P, PACK], BF16, name="grouped", align_bytes=64)
         q_words = sb.tile([P, NQ], U32, name="q_words", align_bytes=64)
         q_scales = sb.tile([P, NQ], U8, name="q_scales", align_bytes=64)
 
-        loads = [(0, 128), (128, 256), (256, 512)]
-        raw = [sb.tile([P, PACK, b - a], F32, name="raw%d" % a) for a, b in loads]
-        q_rows = qT[0].rearrange("(p t) q -> p t q", t=PACK)
-
         nc.vector.memset(pool_scales[:].bitcast(I32), 0)
         nc.sync.dma_start(offsets[:], offs)
-        nc.sync.dma_start(hw_cols[:], hw[0].rearrange("o (p c) -> p (o c)", c=PACK))
-        nc.sync.dma_start(raw[0][:], q_rows[:, :, 0:128])
+        nc.sync.dma_start(weights[:], hw[0].rearrange("o (m c) -> m (o c)", c=GROUPS))
+        nc.sync.dma_start(raw[:], qT[0].rearrange("(p t) q -> p t q", t=PACK))
         scale_rows = k_scales[0].bitcast(I32)
-        for quad in range(4):
-            nc.sync.dma_start(
-                pool_scales[32 * quad : 32 * quad + 4, :].bitcast(I32), scale_rows[4 * quad : 4 * quad + 4, :]
-            )
+        for r in range(4):
+            nc.sync.dma_start(pool_scales[r:P:32, :].bitcast(I32), scale_rows[r:16:4, :])
         nc.sync.dma_start(pool_words[:], k_words[0].rearrange("p n t -> p (n t)").bitcast(I32))
-        nc.sync.dma_start(raw[1][:], q_rows[:, :, 128:256])
-        nc.sync.dma_start(raw[2][:], q_rows[:, :, 256:512])
 
-        make_identity(nc, ident[:])
-        hw_ps = ps.tile([P, PACK, P], F32, name="hw_ps")
-        for c in range(PACK):
-            nc.tensor.transpose(hw_ps[:, c, :], hw_cols[:, c : c + 1].to_broadcast([P, P]), ident[:])
+        nc.vector.memset(ident[:], 0.0)
+        make_identity(nc, ident[:], nomemset=True)
 
-        def interleave(src, a, b):
-            grouped = sb.tile([P, b - a, PACK], BF16, name="grouped%d" % a, align_bytes=64)
-            nc.scalar.copy(out=grouped[:], in_=src.rearrange("p t q -> p q t"))
-            return grouped
-
-        def quantize(grouped, a, b):
-            nc.vector.quantize_mx(
-                out=q_words[:, a:b].bitcast(FP8X4),
-                scales=q_scales[:, a:b],
-                in_=grouped[:].rearrange("p q t -> p (q t)"),
+        src = raw[:].rearrange("p t (m c) -> p m t c", c=GROUPS)
+        dst = grouped[:].rearrange("p c m t -> p m t c")
+        nc.scalar.copy(out=dst[:, :SCALAR_ROWS], in_=src[:, :SCALAR_ROWS])
+        nc.vector.tensor_copy(out=dst[:, SCALAR_ROWS:], in_=src[:, SCALAR_ROWS:])
+        nc.vector.tensor_copy(key_scales[:], pool_scales[:].indirect(offsets[:]))
+        nc.vector.quantize_mx(
+            out=q_words[:].bitcast(FP8X4), scales=q_scales[:], in_=grouped[:].rearrange("p c m t -> p (c m t)")
+        )
+        window = pool_words[:].bitcast(U32)
+        for u in range(2):
+            nc.vector.tensor_copy(
+                key_words[:, u * HALF : (u + 1) * HALF],
+                window.indirect(offsets[:, u * HALF // 16 : (u + 1) * HALF // 16]),
             )
 
-        def scores(name, tiles, a, b):
-            acc = ps.tile([P, len(tiles), b - a], F32, name=name)
-            for n, s in enumerate(tiles):
-                nc.tensor.matmul_mx(
-                    out=acc[:, n, :],
-                    lhsT=key_words[:, s * P : (s + 1) * P].bitcast(FP8X4),
-                    lhsT_scale=key_scales[:, s * P : (s + 1) * P],
-                    rhs=q_words[:, a:b].bitcast(FP8X4),
-                    rhs_scale=q_scales[:, a:b],
-                    start=True,
-                    stop=True,
-                )
+        def scores(u, c):
+            acc = ps.tile([P, HALF], F32, name="acc%d%d" % (u, c), tag="bank%d%d" % (u, c))
+            nc.tensor.matmul_mx(
+                out=acc[:],
+                lhsT=q_words[:, c * P : (c + 1) * P].bitcast(FP8X4),
+                lhsT_scale=q_scales[:, c * P : (c + 1) * P],
+                rhs=key_words[:, u * HALF : (u + 1) * HALF].bitcast(FP8X4),
+                rhs_scale=key_scales[:, u * HALF : (u + 1) * HALF],
+                start=True,
+                stop=True,
+            )
             return acc
 
-        def weigh(name, acc, tiles, a, b):
-            shape = [P, len(tiles), b - a]
-            prod = sb.tile(shape, F32, name=name)
+        def first(u, c):
+            total = sb.tile([P, HALF], F32, name="first%d%d" % (u, c))
+            nc.vector.tensor_scalar(
+                out=total[:], in0=acc[u, c][:], scalar1=0.0, scalar2=weights[:, c : c + 1], op0=ALU.max, op1=ALU.mult
+            )
+            return total
+
+        def relu(u, c):
+            pos = sb.tile([P, HALF], F32, name="pos%d%d" % (u, c))
+            nc.scalar.activation(pos[:], acc[u, c][:], ACT.Relu)
+            return pos
+
+        def add_on(u, c, pos, total):
+            more = sb.tile([P, HALF], F32, name="more%d%d" % (u, c))
             nc.vector.scalar_tensor_tensor(
-                out=prod[:],
-                in0=acc[:],
-                scalar=0.0,
-                in1=hw_rows[:, a:b].unsqueeze(1).to_broadcast(shape),
-                op0=ALU.max,
-                op1=ALU.mult,
+                out=more[:], in0=pos[:], scalar=weights[:, c : c + 1], in1=total[:], op0=ALU.mult, op1=ALU.add
             )
-            return prod
+            return more
 
-        def add_heads(prod, tiles, a, b):
-            nc.vector.tensor_reduce(
-                out=result[:, tiles[0] : tiles[-1] + 1, a // SEG : b // SEG],
-                in_=prod[:].rearrange("p s (j h) -> p s j h", h=SEG),
-                axis=AX.X,
-                op=ALU.add,
-            )
-
-        g0 = interleave(raw[0][:], 0, 128)
-        nc.scalar.copy(out=hw_rows[:].rearrange("m (p c) -> m p c", c=PACK), in_=hw_ps[:].rearrange("m c p -> m p c"))
-        nc.vector.tensor_copy(key_scales[:], pool_scales[:].indirect(offsets[:]))
-        quantize(g0, 0, 128)
-        g1 = interleave(raw[1][:], 128, 256)
-        g2 = interleave(raw[2][:], 256, 512)
-        window = pool_words[:].bitcast(U32)
-        half = N // 2
-        nc.vector.tensor_copy(key_words[:, :half], window.indirect(offsets[:, : half // 16]))
-        acc0a = scores("acc0a", [0, 1], 0, 128)
-        nc.vector.tensor_copy(key_words[:, half:], window.indirect(offsets[:, half // 16 :]))
-        acc0b = scores("acc0b", [2, 3], 0, 128)
-        p0a = weigh("p0a", acc0a, [0, 1], 0, 128)
-        quantize(g1, 128, 256)
-        acc1 = scores("acc1", [0, 1, 2, 3], 128, 256)
-        p0b = weigh("p0b", acc0b, [2, 3], 0, 128)
-        add_heads(p0a, [0, 1], 0, 128)
-        add_heads(p0b, [2, 3], 0, 128)
-        p1 = weigh("p1", acc1, [0, 1, 2, 3], 128, 256)
-        quantize(g2, 256, 512)
-        acc2 = scores("acc2", [0, 1], 256, 512)
-        acc3 = scores("acc3", [2, 3], 256, 512)
-        add_heads(p1, [0, 1, 2, 3], 128, 256)
-        p2 = weigh("p2", acc2, [0, 1], 256, 512)
-        p3 = weigh("p3", acc3, [2, 3], 256, 512)
         rows = out[0].rearrange("(s p) j -> p s j", p=P)
-        add_heads(p2, [0, 1], 256, 512)
-        nc.sync.dma_start(rows[:, 0:2, :], result[:, 0:2, :])
-        add_heads(p3, [2, 3], 256, 512)
-        nc.sync.dma_start(rows[:, 2:4, :], result[:, 2:4, :])
+
+        def finish(u, turned):
+            result = sb.tile([P, 2, NQ // SEG], F32, name="result%d" % u)
+            nc.vector.tensor_reduce(
+                out=result[:], in_=turned[:].rearrange("p s (j h) -> p s j h", h=SEG // GROUPS), axis=AX.X, op=ALU.add
+            )
+            nc.sync.dma_start(rows[:, 2 * u : 2 * u + 2, :], result[:])
+
+        acc = {}
+        for u, c in [(0, 0), (0, 1), (1, 0), (1, 1), (0, 2), (1, 2), (0, 3), (1, 3)]:
+            acc[u, c] = scores(u, c)
+        total = [first(0, 0), first(1, 0)]
+        for c in range(1, GROUPS):
+            for u in range(2):
+                total[u] = add_on(u, c, relu(u, c), total[u])
+        turned = []
+        for u in range(2):
+            tile = ps.tile([P, 2, P], F32, name="turned%d" % u, tag="bank%d0" % u)
+            for s in range(2):
+                nc.tensor.transpose(tile[:, s, :], total[u][:, s * P : (s + 1) * P], ident[:])
+            turned.append(tile)
+        for u in range(2):
+            finish(u, turned[u])

@@ -19,7 +19,7 @@ PACK = 4
 N, T, D, NQ, SEG = 512, 2048, 512, 512, 16
 GROUPS = NQ // P
 HALF = N // 2
-SCALAR_ROWS = 80
+SCALAR_ROWS = 64
 FLOPS = 2 * N * D * NQ
 
 
@@ -42,22 +42,26 @@ def tile_attend_indexer_topk_kernel(tc, qT, k_words, k_scales, hw, offs, out):
         q_scales = sb.tile([P, NQ], U8, name="q_scales", align_bytes=64)
 
         nc.vector.memset(pool_scales[:].bitcast(I32), 0)
+        q_rows = qT[0].rearrange("(p t) q -> p t q", t=PACK)
+        nc.sync.dma_start(raw[:, :2, :], q_rows[:, :2, :])
         nc.sync.dma_start(offsets[:], offs)
-        nc.sync.dma_start(weights[:], hw[0].rearrange("o (m c) -> m (o c)", c=GROUPS))
-        nc.sync.dma_start(raw[:], qT[0].rearrange("(p t) q -> p t q", t=PACK))
         scale_rows = k_scales[0].bitcast(I32)
         for r in range(4):
             nc.sync.dma_start(pool_scales[r:P:32, :].bitcast(I32), scale_rows[r:16:4, :])
+        nc.sync.dma_start(raw[:, 2:, :], q_rows[:, 2:, :])
         nc.sync.dma_start(pool_words[:], k_words[0].rearrange("p n t -> p (n t)").bitcast(I32))
+        nc.sync.dma_start(weights[:], hw[0].rearrange("o (m c) -> m (o c)", c=GROUPS))
 
-        nc.vector.memset(ident[:], 0.0)
+        zero = sb.tile([P, 1], F32, name="zero")
+        nc.vector.memset(zero[:], 0.0)
+        nc.scalar.copy(out=ident[:], in_=zero[:].to_broadcast([P, P]))
         make_identity(nc, ident[:], nomemset=True)
 
         src = raw[:].rearrange("p t (m c) -> p m t c", c=GROUPS)
         dst = grouped[:].rearrange("p c m t -> p m t c")
         nc.scalar.copy(out=dst[:, :SCALAR_ROWS], in_=src[:, :SCALAR_ROWS])
-        nc.vector.tensor_copy(out=dst[:, SCALAR_ROWS:], in_=src[:, SCALAR_ROWS:])
         nc.vector.tensor_copy(key_scales[:], pool_scales[:].indirect(offsets[:]))
+        nc.vector.tensor_copy(out=dst[:, SCALAR_ROWS:], in_=src[:, SCALAR_ROWS:])
         nc.vector.quantize_mx(
             out=q_words[:].bitcast(FP8X4), scales=q_scales[:], in_=grouped[:].rearrange("p c m t -> p (c m t)")
         )

@@ -19,7 +19,7 @@ PACK = 4
 N, T, D, NQ, SEG = 512, 2048, 512, 512, 16
 GROUPS = NQ // P
 HALF = N // 2
-SCALAR_ROWS = 64
+SCALAR_ROWS = 48
 FLOPS = 2 * N * D * NQ
 
 
@@ -113,18 +113,40 @@ def tile_attend_indexer_topk_kernel(tc, qT, k_words, k_scales, hw, offs, out):
             )
             nc.sync.dma_start(rows[:, 2 * u : 2 * u + 2, :], result[:])
 
+        def scaled(u, c, pos):
+            total = sb.tile([P, HALF], F32, name="scaled%d%d" % (u, c))
+            nc.scalar.activation(total[:], pos[:], ACT.Copy, scale=weights[:, c : c + 1])
+            return total
+
         acc = {}
-        for u, c in [(0, 0), (0, 1), (1, 0), (1, 1), (0, 2), (1, 2), (0, 3), (1, 3)]:
-            acc[u, c] = scores(u, c)
-        total = [first(0, 0), first(1, 0)]
-        for c in range(1, GROUPS):
-            for u in range(2):
-                total[u] = add_on(u, c, relu(u, c), total[u])
-        turned = []
         for u in range(2):
+            for c in range(GROUPS):
+                acc[u, c] = scores(u, c)
+        a0 = first(0, 0)
+        pos_a1 = relu(0, 1)
+        a2 = first(0, 2)
+        pos_a3 = relu(0, 3)
+        a01 = add_on(0, 1, pos_a1, a0)
+        a23 = add_on(0, 3, pos_a3, a2)
+        pos_b0 = relu(1, 0)
+        pos_b1 = relu(1, 1)
+        b0 = scaled(1, 0, pos_b0)
+        b2 = first(1, 2)
+        b3 = first(1, 3)
+        b01 = add_on(1, 1, pos_b1, b0)
+        turned = []
+        for u, parts in enumerate([[a01, a23], [b2, b3, b01]]):
             tile = ps.tile([P, 2, P], F32, name="turned%d" % u, tag="bank%d0" % u)
-            for s in range(2):
-                nc.tensor.transpose(tile[:, s, :], total[u][:, s * P : (s + 1) * P], ident[:])
+            for n, part in enumerate(parts):
+                for s in range(2):
+                    nc.tensor.matmul(
+                        tile[:, s, :],
+                        part[:, s * P : (s + 1) * P],
+                        ident[:],
+                        start=(n == 0 and s == 0),
+                        stop=(n == len(parts) - 1 and s == 1),
+                        is_transpose=True,
+                    )
             turned.append(tile)
         for u in range(2):
             finish(u, turned[u])

@@ -72,6 +72,17 @@ def tile_attend_indexer_topk_kernel(tc, qT, k_words, k_scales, hw, offs, out):
                 window.indirect(offsets[:, u * HALF // 16 : (u + 1) * HALF // 16]),
             )
 
+        warm = ps.tile([P, N], F32, name="warm", tag="bank13")
+        nc.tensor.matmul_mx(
+            out=warm[:],
+            lhsT=q_words[:, :P].bitcast(FP8X4),
+            lhsT_scale=q_scales[:, :P],
+            rhs=pool_words[:, :N].bitcast(FP8X4),
+            rhs_scale=pool_scales[:, :N],
+            start=True,
+            stop=True,
+        )
+
         def scores(u, c):
             acc = ps.tile([P, HALF], F32, name="acc%d%d" % (u, c), tag="bank%d%d" % (u, c))
             nc.tensor.matmul_mx(

@@ -34,6 +34,7 @@ def tile_attend_indexer_topk_kernel(tc, qT, k_words, k_scales, hw, offs, out):
         pool_scales = sb.tile([P, T], U8, name="pool_scales", align_bytes=64)
         key_words = sb.tile([P, N], U32, name="key_words", align_bytes=64)
         key_scales = sb.tile([P, N], U8, name="key_scales", align_bytes=64)
+        picked_scales = sb.tile([P, N], U8, name="picked_scales", align_bytes=64)
         weights = sb.tile([P, GROUPS], F32, name="weights")
         ident = sb.tile([P, P], F32, name="ident")
         raw = sb.tile([P, PACK, NQ], F32, name="raw")
@@ -46,8 +47,7 @@ def tile_attend_indexer_topk_kernel(tc, qT, k_words, k_scales, hw, offs, out):
         nc.sync.dma_start(raw[:, :2, :], q_rows[:, :2, :])
         nc.sync.dma_start(offsets[:], offs)
         scale_rows = k_scales[0].bitcast(I32)
-        for r in range(4):
-            nc.sync.dma_start(pool_scales[r:P:32, :].bitcast(I32), scale_rows[r:16:4, :])
+        nc.sync.dma_start(pool_scales[0:P:8, :].bitcast(I32), scale_rows)
         nc.sync.dma_start(raw[:, 2:, :], q_rows[:, 2:, :])
         nc.sync.dma_start(pool_words[:], k_words[0].rearrange("p n t -> p (n t)").bitcast(I32))
         nc.sync.dma_start(weights[:], hw[0].rearrange("o (m c) -> m (o c)", c=GROUPS))
@@ -60,7 +60,13 @@ def tile_attend_indexer_topk_kernel(tc, qT, k_words, k_scales, hw, offs, out):
         src = raw[:].rearrange("p t (m c) -> p m t c", c=GROUPS)
         dst = grouped[:].rearrange("p c m t -> p m t c")
         nc.scalar.copy(out=dst[:, :SCALAR_ROWS], in_=src[:, :SCALAR_ROWS])
-        nc.vector.tensor_copy(key_scales[:], pool_scales[:].indirect(offsets[:]))
+        nc.vector.memset(key_scales[:].bitcast(I32), 0)
+        nc.vector.tensor_copy(picked_scales[:], pool_scales[:].indirect(offsets[:]))
+        for quad in range(4):
+            nc.sync.dma_start(
+                key_scales[32 * quad : 32 * quad + 4, :].bitcast(I32),
+                picked_scales[32 * quad : 32 * quad + 32 : 8, :].bitcast(I32),
+            )
         nc.vector.tensor_copy(out=dst[:, SCALAR_ROWS:], in_=src[:, SCALAR_ROWS:])
         nc.vector.quantize_mx(
             out=q_words[:].bitcast(FP8X4), scales=q_scales[:], in_=grouped[:].rearrange("p c m t -> p (c m t)")
@@ -71,17 +77,6 @@ def tile_attend_indexer_topk_kernel(tc, qT, k_words, k_scales, hw, offs, out):
                 key_words[:, u * HALF : (u + 1) * HALF],
                 window.indirect(offsets[:, u * HALF // 16 : (u + 1) * HALF // 16]),
             )
-
-        warm = ps.tile([P, N], F32, name="warm", tag="bank13")
-        nc.tensor.matmul_mx(
-            out=warm[:],
-            lhsT=q_words[:, :P].bitcast(FP8X4),
-            lhsT_scale=q_scales[:, :P],
-            rhs=pool_words[:, :N].bitcast(FP8X4),
-            rhs_scale=pool_scales[:, :N],
-            start=True,
-            stop=True,
-        )
 
         def scores(u, c):
             acc = ps.tile([P, HALF], F32, name="acc%d%d" % (u, c), tag="bank%d%d" % (u, c))
@@ -129,6 +124,25 @@ def tile_attend_indexer_topk_kernel(tc, qT, k_words, k_scales, hw, offs, out):
             nc.scalar.activation(total[:], pos[:], ACT.Copy, scale=weights[:, c : c + 1])
             return total
 
+        def pooled(u, c, pos):
+            total = sb.tile([P, HALF], F32, name="pooled%d%d" % (u, c))
+            nc.gpsimd.tensor_scalar(
+                out=total[:], in0=pos[:], scalar1=weights[:, c : c + 1], scalar2=zero[:], op0=ALU.mult, op1=ALU.add
+            )
+            return total
+
+        def turn(tile, parts, blocks):
+            for n, part in enumerate(parts):
+                for k, s in enumerate(blocks):
+                    nc.tensor.matmul(
+                        tile[:, k, :],
+                        part[:, s * P : (s + 1) * P],
+                        ident[:],
+                        start=(n == 0 and k == 0),
+                        stop=(n == len(parts) - 1 and k == len(blocks) - 1),
+                        is_transpose=True,
+                    )
+
         acc = {}
         for u in range(2):
             for c in range(GROUPS):
@@ -140,24 +154,15 @@ def tile_attend_indexer_topk_kernel(tc, qT, k_words, k_scales, hw, offs, out):
         a01 = add_on(0, 1, pos_a1, a0)
         a23 = add_on(0, 3, pos_a3, a2)
         pos_b0 = relu(1, 0)
-        pos_b1 = relu(1, 1)
-        b0 = scaled(1, 0, pos_b0)
-        b2 = first(1, 2)
+        b1 = first(1, 1)
+        pos_b2 = relu(1, 2)
+        b0 = pooled(1, 0, pos_b0)
         b3 = first(1, 3)
-        b01 = add_on(1, 1, pos_b1, b0)
+        b2 = scaled(1, 2, pos_b2)
         turned = []
-        for u, parts in enumerate([[a01, a23], [b2, b3, b01]]):
+        for u, parts in enumerate([[a01, a23], [b1, b0, b3, b2]]):
             tile = ps.tile([P, 2, P], F32, name="turned%d" % u, tag="bank%d0" % u)
-            for n, part in enumerate(parts):
-                for s in range(2):
-                    nc.tensor.matmul(
-                        tile[:, s, :],
-                        part[:, s * P : (s + 1) * P],
-                        ident[:],
-                        start=(n == 0 and s == 0),
-                        stop=(n == len(parts) - 1 and s == 1),
-                        is_transpose=True,
-                    )
+            turn(tile, parts, range(2))
             turned.append(tile)
         for u in range(2):
             finish(u, turned[u])

@@ -143,6 +143,16 @@ def tile_attend_indexer_topk_kernel(tc, qT, k_words, k_scales, hw, offs, out):
                         is_transpose=True,
                     )
 
+        warm = ps.tile([P, N], F32, name="warm", tag="bank13")
+        nc.tensor.matmul_mx(
+            out=warm[:],
+            lhsT=q_words[:, :P].bitcast(FP8X4),
+            lhsT_scale=q_scales[:, :P],
+            rhs=window[:, :N].bitcast(FP8X4),
+            rhs_scale=q_scales[:],
+            start=True,
+            stop=True,
+        )
         acc = {}
         for u in range(2):
             for c in range(GROUPS):
@@ -152,15 +162,14 @@ def tile_attend_indexer_topk_kernel(tc, qT, k_words, k_scales, hw, offs, out):
         a2 = first(0, 2)
         pos_a3 = relu(0, 3)
         a01 = add_on(0, 1, pos_a1, a0)
-        a23 = add_on(0, 3, pos_a3, a2)
-        pos_b0 = relu(1, 0)
-        b1 = first(1, 1)
-        pos_b2 = relu(1, 2)
-        b0 = pooled(1, 0, pos_b0)
+        a3 = pooled(0, 3, pos_a3)
+        b0 = first(1, 0)
+        pos_b1 = relu(1, 1)
+        b2 = first(1, 2)
+        b1 = scaled(1, 1, pos_b1)
         b3 = first(1, 3)
-        b2 = scaled(1, 2, pos_b2)
         turned = []
-        for u, parts in enumerate([[a01, a23], [b1, b0, b3, b2]]):
+        for u, parts in enumerate([[a2, a01, a3], [b0, b2, b1, b3]]):
             tile = ps.tile([P, 2, P], F32, name="turned%d" % u, tag="bank%d0" % u)
             turn(tile, parts, range(2))
             turned.append(tile)

@@ -91,16 +91,22 @@ def tile_attend_indexer_topk_kernel(tc, qT, k_words, k_scales, hw, offs, out):
             )
             return acc
 
+        def by_parity(tile):
+            return tile[:].rearrange("p (s e) -> p e s", e=2)
+
+        def parted(tile):
+            return tile[:].rearrange("p (e s) -> p e s", e=2)
+
         def first(u, c):
             total = sb.tile([P, HALF], F32, name="first%d%d" % (u, c))
             nc.vector.tensor_scalar(
-                out=total[:], in0=acc[u, c][:], scalar1=0.0, scalar2=weights[:, c : c + 1], op0=ALU.max, op1=ALU.mult
+                out=parted(total), in0=by_parity(acc[u, c]), scalar1=0.0, scalar2=weights[:, c : c + 1], op0=ALU.max, op1=ALU.mult
             )
             return total
 
         def relu(u, c):
             pos = sb.tile([P, HALF], F32, name="pos%d%d" % (u, c))
-            nc.scalar.activation(pos[:], acc[u, c][:], ACT.Relu)
+            nc.scalar.activation(parted(pos), by_parity(acc[u, c]), ACT.Relu)
             return pos
 
         def add_on(u, c, pos, total):
@@ -110,14 +116,14 @@ def tile_attend_indexer_topk_kernel(tc, qT, k_words, k_scales, hw, offs, out):
             )
             return more
 
-        rows = out[0].rearrange("(s p) j -> p s j", p=P)
+        rows = out[0].rearrange("(u p e) j -> u p e j", p=P, e=2)
 
         def finish(u, turned):
             result = sb.tile([P, 2, NQ // SEG], F32, name="result%d" % u)
             nc.vector.tensor_reduce(
                 out=result[:], in_=turned[:].rearrange("p s (j h) -> p s j h", h=SEG // GROUPS), axis=AX.X, op=ALU.add
             )
-            nc.sync.dma_start(rows[:, 2 * u : 2 * u + 2, :], result[:])
+            nc.sync.dma_start(rows[u], result[:])
 
         def scaled(u, c, pos):
             total = sb.tile([P, HALF], F32, name="scaled%d%d" % (u, c))
@@ -168,10 +174,24 @@ def tile_attend_indexer_topk_kernel(tc, qT, k_words, k_scales, hw, offs, out):
         b2 = first(1, 2)
         b1 = scaled(1, 1, pos_b1)
         b3 = first(1, 3)
-        turned = []
-        for u, parts in enumerate([[a2, a01, a3], [b0, b2, b1, b3]]):
-            tile = ps.tile([P, 2, P], F32, name="turned%d" % u, tag="bank%d0" % u)
-            turn(tile, parts, range(2))
-            turned.append(tile)
-        for u in range(2):
-            finish(u, turned[u])
+        turned = ps.tile([P, 2, P], F32, name="turned0", tag="bank00")
+        turn(turned, [a2, a01, a3], range(2))
+        last = [ps.tile([P, P], F32, name="last%d" % s, tag="bank1%d" % s) for s in range(2)]
+        parts = [b0, b2, b1, b3]
+        for n, part in enumerate(parts):
+            for s in range(2):
+                nc.tensor.matmul(
+                    last[s][:],
+                    part[:, s * P : (s + 1) * P],
+                    ident[:],
+                    start=(n == 0),
+                    stop=(n == len(parts) - 1),
+                    is_transpose=True,
+                )
+        finish(0, turned)
+        result = sb.tile([P, 2, NQ // SEG], F32, name="result1")
+        for s in range(2):
+            nc.vector.tensor_reduce(
+                out=result[:, s, :], in_=last[s][:].rearrange("p (j h) -> p j h", h=SEG // GROUPS), axis=AX.X, op=ALU.add
+            )
+        nc.sync.dma_start(rows[1], result[:])

@@ -137,18 +137,6 @@ def tile_attend_indexer_topk_kernel(tc, qT, k_words, k_scales, hw, offs, out):
             )
             return total
 
-        def turn(tile, parts, blocks):
-            for n, part in enumerate(parts):
-                for k, s in enumerate(blocks):
-                    nc.tensor.matmul(
-                        tile[:, k, :],
-                        part[:, s * P : (s + 1) * P],
-                        ident[:],
-                        start=(n == 0 and k == 0),
-                        stop=(n == len(parts) - 1 and k == len(blocks) - 1),
-                        is_transpose=True,
-                    )
-
         warm = ps.tile([P, N], F32, name="warm", tag="bank13")
         nc.tensor.matmul_mx(
             out=warm[:],
@@ -169,25 +157,46 @@ def tile_attend_indexer_topk_kernel(tc, qT, k_words, k_scales, hw, offs, out):
         pos_a3 = relu(0, 3)
         a01 = add_on(0, 1, pos_a1, a0)
         a3 = pooled(0, 3, pos_a3)
-        b0 = first(1, 0)
-        pos_b1 = relu(1, 1)
+        pos_b0 = relu(1, 0)
+        b0 = scaled(1, 0, pos_b0)
+        b1 = first(1, 1)
         b2 = first(1, 2)
-        b1 = scaled(1, 1, pos_b1)
-        b3 = first(1, 3)
+        b3 = sb.tile([P, HALF], F32, name="first13")
+        for e in range(2):
+            nc.vector.tensor_scalar(
+                out=parted(b3)[:, e, :],
+                in0=by_parity(acc[1, 3])[:, e, :],
+                scalar1=0.0,
+                scalar2=weights[:, 3:4],
+                op0=ALU.max,
+                op1=ALU.mult,
+            )
         turned = ps.tile([P, 2, P], F32, name="turned0", tag="bank00")
-        turn(turned, [a2, a01, a3], range(2))
-        last = [ps.tile([P, P], F32, name="last%d" % s, tag="bank1%d" % s) for s in range(2)]
-        parts = [b0, b2, b1, b3]
-        for n, part in enumerate(parts):
-            for s in range(2):
+        last = [ps.tile([P, P], F32, name="last%d" % s, tag="bank0%d" % (s + 1)) for s in range(2)]
+
+        def turn_first(part):
+            for e in range(2):
                 nc.tensor.matmul(
-                    last[s][:],
-                    part[:, s * P : (s + 1) * P],
+                    turned[:, e, :],
+                    part[:, e * P : (e + 1) * P],
                     ident[:],
-                    start=(n == 0),
-                    stop=(n == len(parts) - 1),
+                    start=part is a2 and e == 0,
+                    stop=part is a3 and e == 1,
                     is_transpose=True,
                 )
+
+        def turn_last(part, e):
+            nc.tensor.matmul(
+                last[e][:], part[:, e * P : (e + 1) * P], ident[:], start=part is b1, stop=part is b3, is_transpose=True
+            )
+
+        turn_first(a2)
+        turn_first(a01)
+        turn_last(b1, 0)
+        turn_last(b1, 1)
+        turn_first(a3)
+        for part, e in [(b0, 0), (b0, 1), (b2, 0), (b3, 0), (b2, 1), (b3, 1)]:
+            turn_last(part, e)
         finish(0, turned)
         result = sb.tile([P, 2, NQ // SEG], F32, name="result1")
         for s in range(2):

@@ -137,16 +137,6 @@ def tile_attend_indexer_topk_kernel(tc, qT, k_words, k_scales, hw, offs, out):
             )
             return total
 
-        warm = ps.tile([P, N], F32, name="warm", tag="bank13")
-        nc.tensor.matmul_mx(
-            out=warm[:],
-            lhsT=q_words[:, :P].bitcast(FP8X4),
-            lhsT_scale=q_scales[:, :P],
-            rhs=window[:, :N].bitcast(FP8X4),
-            rhs_scale=q_scales[:],
-            start=True,
-            stop=True,
-        )
         acc = {}
         for u in range(2):
             for c in range(GROUPS):

@@ -17,8 +17,9 @@ ACT = mybir.ActivationFunctionType
 P = 128
 PACK = 4
 N, T, D, NQ, SEG = 512, 2048, 512, 512, 16
-GROUPS = NQ // P
 HALF = N // 2
+QHALF = NQ // 2
+RUNS = NQ // SEG
 SCALAR_ROWS = 48
 FLOPS = 2 * N * D * NQ
 
@@ -34,43 +35,49 @@ def tile_attend_indexer_topk_kernel(tc, qT, k_words, k_scales, hw, offs, out):
         pool_scales = sb.tile([P, T], U8, name="pool_scales", align_bytes=64)
         key_words = sb.tile([P, N], U32, name="key_words", align_bytes=64)
         key_scales = sb.tile([P, N], U8, name="key_scales", align_bytes=64)
-        picked_scales = sb.tile([P, N], U8, name="picked_scales", align_bytes=64)
-        weights = sb.tile([P, GROUPS], F32, name="weights")
+        weight_rows = sb.tile([P, QHALF], F32, name="weight_rows")
+        weights = sb.tile([P, 2, 2], F32, name="weights")
         ident = sb.tile([P, P], F32, name="ident")
-        raw = sb.tile([P, PACK, NQ], F32, name="raw")
-        grouped = sb.tile([P, GROUPS, P, PACK], BF16, name="grouped", align_bytes=64)
+        raw_a = sb.tile([P, PACK, QHALF], F32, name="raw_a")
+        grouped = [sb.tile([P, 2, P, PACK], BF16, name="grouped%d" % x, align_bytes=64) for x in range(2)]
         q_words = sb.tile([P, NQ], U32, name="q_words", align_bytes=64)
         q_scales = sb.tile([P, NQ], U8, name="q_scales", align_bytes=64)
 
         nc.vector.memset(pool_scales[:].bitcast(I32), 0)
+        nc.gpsimd.memset(weight_rows[:], 0.0)
         q_rows = qT[0].rearrange("(p t) q -> p t q", t=PACK)
-        nc.sync.dma_start(raw[:, :2, :], q_rows[:, :2, :])
+        raw_b = sb.tile([P, PACK, QHALF], F32, name="raw_b", tag="second")
+        nc.sync.dma_start(raw_a[:], q_rows[:, :, :QHALF])
         nc.sync.dma_start(offsets[:], offs)
-        scale_rows = k_scales[0].bitcast(I32)
-        nc.sync.dma_start(pool_scales[0:P:8, :].bitcast(I32), scale_rows)
-        nc.sync.dma_start(raw[:, 2:, :], q_rows[:, 2:, :])
+        for quad in range(4):
+            nc.sync.dma_start(
+                pool_scales[32 * quad : 32 * quad + 4, :].bitcast(I32), k_scales[0, 4 * quad : 4 * quad + 4].bitcast(I32)
+            )
+        nc.sync.dma_start(weight_rows[0:2, :], hw[0].rearrange("o (x q) -> (o x) q", x=2))
         nc.sync.dma_start(pool_words[:], k_words[0].rearrange("p n t -> p (n t)").bitcast(I32))
-        nc.sync.dma_start(weights[:], hw[0].rearrange("o (m c) -> m (o c)", c=GROUPS))
+        nc.sync.dma_start(raw_b[:], q_rows[:, :, QHALF:])
 
         zero = sb.tile([P, 1], F32, name="zero")
         nc.vector.memset(zero[:], 0.0)
         nc.scalar.copy(out=ident[:], in_=zero[:].to_broadcast([P, P]))
         make_identity(nc, ident[:], nomemset=True)
 
-        src = raw[:].rearrange("p t (m c) -> p m t c", c=GROUPS)
-        dst = grouped[:].rearrange("p c m t -> p m t c")
+        src = raw_a[:].rearrange("p t (m c) -> p m t c", c=2)
+        dst = grouped[0][:].rearrange("p c m t -> p m t c")
         nc.scalar.copy(out=dst[:, :SCALAR_ROWS], in_=src[:, :SCALAR_ROWS])
-        nc.vector.memset(key_scales[:].bitcast(I32), 0)
-        nc.vector.tensor_copy(picked_scales[:], pool_scales[:].indirect(offsets[:]))
-        for quad in range(4):
-            nc.sync.dma_start(
-                key_scales[32 * quad : 32 * quad + 4, :].bitcast(I32),
-                picked_scales[32 * quad : 32 * quad + 32 : 8, :].bitcast(I32),
-            )
         nc.vector.tensor_copy(out=dst[:, SCALAR_ROWS:], in_=src[:, SCALAR_ROWS:])
+        nc.vector.tensor_copy(key_scales[:], pool_scales[:].indirect(offsets[:]))
         nc.vector.quantize_mx(
-            out=q_words[:].bitcast(FP8X4), scales=q_scales[:], in_=grouped[:].rearrange("p c m t -> p (c m t)")
+            out=q_words[:, :QHALF].bitcast(FP8X4),
+            scales=q_scales[:, :QHALF],
+            in_=grouped[0][:].rearrange("p c m t -> p (c m t)"),
         )
+
+        turned_weights = ps.tile([P, 2, P], F32, name="turned_weights", tag="bank7")
+        for c in range(2):
+            nc.tensor.transpose(turned_weights[:, c, :], weight_rows[:, c:QHALF:2], ident[:])
+        nc.scalar.copy(out=weights[:], in_=turned_weights[:, :, 0:2])
+
         window = pool_words[:].bitcast(U32)
         for u in range(2):
             nc.vector.tensor_copy(
@@ -78,12 +85,13 @@ def tile_attend_indexer_topk_kernel(tc, qT, k_words, k_scales, hw, offs, out):
                 window.indirect(offsets[:, u * HALF // 16 : (u + 1) * HALF // 16]),
             )
 
-        def scores(u, c):
-            acc = ps.tile([P, HALF], F32, name="acc%d%d" % (u, c), tag="bank%d%d" % (u, c))
+        def scores(x, u, c):
+            acc = ps.tile([P, HALF], F32, name="acc%d%d%d" % (x, u, c), tag="bank%d" % (4 * x + 2 * u + c))
+            cols = slice((2 * x + c) * P, (2 * x + c + 1) * P)
             nc.tensor.matmul_mx(
                 out=acc[:],
-                lhsT=q_words[:, c * P : (c + 1) * P].bitcast(FP8X4),
-                lhsT_scale=q_scales[:, c * P : (c + 1) * P],
+                lhsT=q_words[:, cols].bitcast(FP8X4),
+                lhsT_scale=q_scales[:, cols],
                 rhs=key_words[:, u * HALF : (u + 1) * HALF].bitcast(FP8X4),
                 rhs_scale=key_scales[:, u * HALF : (u + 1) * HALF],
                 start=True,
@@ -97,100 +105,108 @@ def tile_attend_indexer_topk_kernel(tc, qT, k_words, k_scales, hw, offs, out):
         def parted(tile):
             return tile[:].rearrange("p (e s) -> p e s", e=2)
 
-        def first(u, c):
-            total = sb.tile([P, HALF], F32, name="first%d%d" % (u, c))
+        def weight(x, c):
+            return weights[:, c, x : x + 1]
+
+        def fresh(kind, x, u, c):
+            if x == 0 and kind in ("first", "pos"):
+                return held[:, 2 * u + c, :]
+            return sb.tile([P, HALF], F32, name="%s%d%d%d" % (kind, x, u, c))
+
+        def first(x, u, c):
+            total = fresh("first", x, u, c)
             nc.vector.tensor_scalar(
-                out=parted(total), in0=by_parity(acc[u, c]), scalar1=0.0, scalar2=weights[:, c : c + 1], op0=ALU.max, op1=ALU.mult
+                out=parted(total), in0=by_parity(acc[x, u, c]), scalar1=0.0, scalar2=weight(x, c), op0=ALU.max, op1=ALU.mult
             )
             return total
 
-        def relu(u, c):
-            pos = sb.tile([P, HALF], F32, name="pos%d%d" % (u, c))
-            nc.scalar.activation(parted(pos), by_parity(acc[u, c]), ACT.Relu)
+        def relu(x, u, c):
+            pos = fresh("pos", x, u, c)
+            nc.scalar.activation(parted(pos), by_parity(acc[x, u, c]), ACT.Relu)
             return pos
 
-        def add_on(u, c, pos, total):
-            more = sb.tile([P, HALF], F32, name="more%d%d" % (u, c))
-            nc.vector.scalar_tensor_tensor(
-                out=more[:], in0=pos[:], scalar=weights[:, c : c + 1], in1=total[:], op0=ALU.mult, op1=ALU.add
-            )
-            return more
+        def scaled(x, u, c, pos):
+            total = fresh("scaled", x, u, c)
+            nc.scalar.activation(total[:], pos[:], ACT.Copy, scale=weight(x, c))
+            return total
 
+        def pooled(x, u, c, pos):
+            total = fresh("pooled", x, u, c)
+            nc.gpsimd.tensor_scalar(
+                out=total[:], in0=pos[:], scalar1=weight(x, c), scalar2=zero[:], op0=ALU.mult, op1=ALU.add
+            )
+            return total
+
+        def prepare(engine_copy, c):
+            engine_copy(out=grouped[1][:, c], in_=raw_b[:].rearrange("p t (m c) -> p c m t", c=2)[:, c])
+
+        def quantise(c):
+            cols = slice((2 + c) * P, (3 + c) * P)
+            nc.vector.quantize_mx(
+                out=q_words[:, cols].bitcast(FP8X4),
+                scales=q_scales[:, cols],
+                in_=grouped[1][:, c].rearrange("p m t -> p (m t)"),
+            )
+
+        def turn(bank, part, e, start, stop):
+            nc.tensor.matmul(bank, part[:, e * P : (e + 1) * P], ident[:], start=start, stop=stop, is_transpose=True)
+
+        result = [sb.tile([P, 2, RUNS], F32, name="result%d" % u) for u in range(2)]
         rows = out[0].rearrange("(u p e) j -> u p e j", p=P, e=2)
 
-        def finish(u, turned):
-            result = sb.tile([P, 2, NQ // SEG], F32, name="result%d" % u)
-            nc.vector.tensor_reduce(
-                out=result[:], in_=turned[:].rearrange("p s (j h) -> p s j h", h=SEG // GROUPS), axis=AX.X, op=ALU.add
-            )
-            nc.sync.dma_start(rows[u], result[:])
-
-        def scaled(u, c, pos):
-            total = sb.tile([P, HALF], F32, name="scaled%d%d" % (u, c))
-            nc.scalar.activation(total[:], pos[:], ACT.Copy, scale=weights[:, c : c + 1])
-            return total
-
-        def pooled(u, c, pos):
-            total = sb.tile([P, HALF], F32, name="pooled%d%d" % (u, c))
-            nc.gpsimd.tensor_scalar(
-                out=total[:], in0=pos[:], scalar1=weights[:, c : c + 1], scalar2=zero[:], op0=ALU.mult, op1=ALU.add
-            )
-            return total
+        def fold(dest, bank):
+            nc.vector.tensor_reduce(out=dest, in_=bank, axis=AX.X, op=ALU.add)
 
         acc = {}
         for u in range(2):
-            for c in range(GROUPS):
-                acc[u, c] = scores(u, c)
-        a0 = first(0, 0)
-        pos_a1 = relu(0, 1)
-        a2 = first(0, 2)
-        pos_a3 = relu(0, 3)
-        a01 = add_on(0, 1, pos_a1, a0)
-        a3 = pooled(0, 3, pos_a3)
-        pos_b0 = relu(1, 0)
-        b0 = scaled(1, 0, pos_b0)
-        b1 = first(1, 1)
-        b2 = first(1, 2)
-        b3 = sb.tile([P, HALF], F32, name="first13")
+            for c in range(2):
+                acc[0, u, c] = scores(0, u, c)
+        prepare(nc.vector.tensor_copy, 0)
+        prepare(nc.scalar.copy, 1)
+        quantise(0)
+        quantise(1)
+        held = sb.tile([P, 4, HALF], F32, name="held", tag="second")
+        for u in range(2):
+            for c in range(2):
+                acc[1, u, c] = scores(1, u, c)
+        pos_a00 = relu(0, 0, 0)
+        pos_a10 = relu(0, 1, 0)
+        a01 = first(0, 0, 1)
+        a11 = first(0, 1, 1)
+        a00 = pooled(0, 0, 0, pos_a00)
+        a10 = scaled(0, 1, 0, pos_a10)
+        pos_b00 = relu(1, 0, 0)
+        b00 = pooled(1, 0, 0, pos_b00)
+        b01 = first(1, 0, 1)
+        pos_b10 = relu(1, 1, 0)
+        b10 = scaled(1, 1, 0, pos_b10)
+        b11 = fresh("first", 1, 1, 1)
         for e in range(2):
             nc.vector.tensor_scalar(
-                out=parted(b3)[:, e, :],
-                in0=by_parity(acc[1, 3])[:, e, :],
+                out=parted(b11)[:, e, :],
+                in0=by_parity(acc[1, 1, 1])[:, e, :],
                 scalar1=0.0,
-                scalar2=weights[:, 3:4],
+                scalar2=weight(1, 1),
                 op0=ALU.max,
                 op1=ALU.mult,
             )
-        turned = ps.tile([P, 2, P], F32, name="turned0", tag="bank00")
-        last = [ps.tile([P, P], F32, name="last%d" % s, tag="bank0%d" % (s + 1)) for s in range(2)]
-
-        def turn_first(part):
+        turned_a = [ps.tile([P, 2, P], F32, name="turned_a%d" % u, tag="bank%d" % u) for u in range(2)]
+        for u, parts in enumerate(((a01, a00), (a11, a10))):
+            for part in parts:
+                for e in range(2):
+                    turn(turned_a[u][:, e, :], part, e, part is parts[0] and e == 0, part is parts[1] and e == 1)
+        turned_b = ps.tile([P, 2, P], F32, name="turned_b", tag="bank2")
+        for part in (b00, b01):
             for e in range(2):
-                nc.tensor.matmul(
-                    turned[:, e, :],
-                    part[:, e * P : (e + 1) * P],
-                    ident[:],
-                    start=part is a2 and e == 0,
-                    stop=part is a3 and e == 1,
-                    is_transpose=True,
-                )
-
-        def turn_last(part, e):
-            nc.tensor.matmul(
-                last[e][:], part[:, e * P : (e + 1) * P], ident[:], start=part is b1, stop=part is b3, is_transpose=True
-            )
-
-        turn_first(a2)
-        turn_first(a01)
-        turn_last(b1, 0)
-        turn_last(b1, 1)
-        turn_first(a3)
-        for part, e in [(b0, 0), (b0, 1), (b2, 0), (b3, 0), (b2, 1), (b3, 1)]:
-            turn_last(part, e)
-        finish(0, turned)
-        result = sb.tile([P, 2, NQ // SEG], F32, name="result1")
-        for s in range(2):
-            nc.vector.tensor_reduce(
-                out=result[:, s, :], in_=last[s][:].rearrange("p (j h) -> p j h", h=SEG // GROUPS), axis=AX.X, op=ALU.add
-            )
-        nc.sync.dma_start(rows[1], result[:])
+                turn(turned_b[:, e, :], part, e, part is b00 and e == 0, part is b01 and e == 1)
+        last = [ps.tile([P, P], F32, name="last%d" % e, tag="bank%d" % (3 + e)) for e in range(2)]
+        for part in (b10, b11):
+            for e in range(2):
+                turn(last[e][:], part, e, part is b10, part is b11)
+        for u in range(2):
+            fold(result[u][:, :, : RUNS // 2], turned_a[u][:].rearrange("p e (j h) -> p e j h", h=SEG // 2))
+        fold(result[0][:, :, RUNS // 2 :], turned_b[:].rearrange("p e (j h) -> p e j h", h=SEG // 2))
+        nc.sync.dma_start(rows[0], result[0][:])
+        for e in range(2):
+            fold(result[1][:, e, RUNS // 2 :], last[e][:].rearrange("p (j h) -> p j h", h=SEG // 2))
+        nc.sync.dma_start(rows[1], result[1][:])

@@ -21,6 +21,7 @@ HALF = N // 2
 QHALF = NQ // 2
 RUNS = NQ // SEG
 SCALAR_ROWS = 48
+LATE_SCALAR_ROWS = 88
 FLOPS = 2 * N * D * NQ
 
 
@@ -78,6 +79,16 @@ def tile_attend_indexer_topk_kernel(tc, qT, k_words, k_scales, hw, offs, out):
             nc.tensor.transpose(turned_weights[:, c, :], weight_rows[:, c:QHALF:2], ident[:])
         nc.scalar.copy(out=weights[:], in_=turned_weights[:, :, 0:2])
 
+        warm = ps.tile([P, N], F32, name="warm", tag="bank7")
+        nc.tensor.matmul_mx(
+            out=warm[:],
+            lhsT=q_words[:, :P].bitcast(FP8X4),
+            lhsT_scale=q_scales[:, :P],
+            rhs=pool_words[:, :N].bitcast(FP8X4),
+            rhs_scale=key_scales[:],
+            start=True,
+            stop=True,
+        )
         window = pool_words[:].bitcast(U32)
         for u in range(2):
             nc.vector.tensor_copy(
@@ -137,8 +148,8 @@ def tile_attend_indexer_topk_kernel(tc, qT, k_words, k_scales, hw, offs, out):
             )
             return total
 
-        def prepare(engine_copy, c):
-            engine_copy(out=grouped[1][:, c], in_=raw_b[:].rearrange("p t (m c) -> p c m t", c=2)[:, c])
+        def prepare(engine_copy, c, rows):
+            engine_copy(out=grouped[1][:, c, rows], in_=raw_b[:].rearrange("p t (m c) -> p c m t", c=2)[:, c, rows])
 
         def quantise(c):
             cols = slice((2 + c) * P, (3 + c) * P)
@@ -161,13 +172,14 @@ def tile_attend_indexer_topk_kernel(tc, qT, k_words, k_scales, hw, offs, out):
         for u in range(2):
             for c in range(2):
                 acc[0, u, c] = scores(0, u, c)
-        prepare(nc.vector.tensor_copy, 0)
-        prepare(nc.scalar.copy, 1)
+        prepare(nc.vector.tensor_copy, 0, slice(0, P))
+        prepare(nc.scalar.copy, 1, slice(0, LATE_SCALAR_ROWS))
+        prepare(nc.vector.tensor_copy, 1, slice(LATE_SCALAR_ROWS, P))
         quantise(0)
         quantise(1)
         held = sb.tile([P, 4, HALF], F32, name="held", tag="second")
-        for u in range(2):
-            for c in range(2):
+        for c in range(2):
+            for u in range(2):
                 acc[1, u, c] = scores(1, u, c)
         pos_a00 = relu(0, 0, 0)
         pos_a10 = relu(0, 1, 0)
@@ -177,9 +189,9 @@ def tile_attend_indexer_topk_kernel(tc, qT, k_words, k_scales, hw, offs, out):
         a10 = scaled(0, 1, 0, pos_a10)
         pos_b00 = relu(1, 0, 0)
         b00 = pooled(1, 0, 0, pos_b00)
-        b01 = first(1, 0, 1)
         pos_b10 = relu(1, 1, 0)
         b10 = scaled(1, 1, 0, pos_b10)
+        b01 = first(1, 0, 1)
         b11 = fresh("first", 1, 1, 1)
         for e in range(2):
             nc.vector.tensor_scalar(

@@ -162,7 +162,7 @@ def tile_attend_indexer_topk_kernel(tc, qT, k_words, k_scales, hw, offs, out):
         def turn(bank, part, e, start, stop):
             nc.tensor.matmul(bank, part[:, e * P : (e + 1) * P], ident[:], start=start, stop=stop, is_transpose=True)
 
-        result = [sb.tile([P, 2, RUNS], F32, name="result%d" % u) for u in range(2)]
+        result = sb.tile([P, 2, 2, RUNS], F32, name="result")
         rows = out[0].rearrange("(u p e) j -> u p e j", p=P, e=2)
 
         def fold(dest, bank):
@@ -178,8 +178,8 @@ def tile_attend_indexer_topk_kernel(tc, qT, k_words, k_scales, hw, offs, out):
         quantise(0)
         quantise(1)
         held = sb.tile([P, 4, HALF], F32, name="held", tag="second")
-        for c in range(2):
-            for u in range(2):
+        for u in range(2):
+            for c in range(2):
                 acc[1, u, c] = scores(1, u, c)
         pos_a00 = relu(0, 0, 0)
         pos_a10 = relu(0, 1, 0)
@@ -189,36 +189,20 @@ def tile_attend_indexer_topk_kernel(tc, qT, k_words, k_scales, hw, offs, out):
         a10 = scaled(0, 1, 0, pos_a10)
         pos_b00 = relu(1, 0, 0)
         b00 = pooled(1, 0, 0, pos_b00)
+        b01 = first(1, 0, 1)
         pos_b10 = relu(1, 1, 0)
         b10 = scaled(1, 1, 0, pos_b10)
-        b01 = first(1, 0, 1)
-        b11 = fresh("first", 1, 1, 1)
-        for e in range(2):
-            nc.vector.tensor_scalar(
-                out=parted(b11)[:, e, :],
-                in0=by_parity(acc[1, 1, 1])[:, e, :],
-                scalar1=0.0,
-                scalar2=weight(1, 1),
-                op0=ALU.max,
-                op1=ALU.mult,
-            )
-        turned_a = [ps.tile([P, 2, P], F32, name="turned_a%d" % u, tag="bank%d" % u) for u in range(2)]
-        for u, parts in enumerate(((a01, a00), (a11, a10))):
+        b11 = first(1, 1, 1)
+        turned_a = ps.tile([P, 2, 2, P], F32, name="turned_a", tag="bank0")
+        for u, part in ((0, a01), (1, a11), (0, a00), (1, a10)):
+            for e in range(2):
+                turn(turned_a[:, u, e, :], part, e, part is a01 and e == 0, part is a10 and e == 1)
+        turned_b = [ps.tile([P, 2, P], F32, name="turned_b%d" % u, tag="bank%d" % (1 + u)) for u in range(2)]
+        for u, parts in enumerate(((b01, b00), (b11, b10))):
             for part in parts:
                 for e in range(2):
-                    turn(turned_a[u][:, e, :], part, e, part is parts[0] and e == 0, part is parts[1] and e == 1)
-        turned_b = ps.tile([P, 2, P], F32, name="turned_b", tag="bank2")
-        for part in (b00, b01):
-            for e in range(2):
-                turn(turned_b[:, e, :], part, e, part is b00 and e == 0, part is b01 and e == 1)
-        last = [ps.tile([P, P], F32, name="last%d" % e, tag="bank%d" % (3 + e)) for e in range(2)]
-        for part in (b10, b11):
-            for e in range(2):
-                turn(last[e][:], part, e, part is b10, part is b11)
+                    turn(turned_b[u][:, e, :], part, e, part is parts[0] and e == 0, part is parts[1] and e == 1)
+        fold(result[:, :, :, : RUNS // 2], turned_a[:].rearrange("p u e (j h) -> p u e j h", h=SEG // 2))
         for u in range(2):
-            fold(result[u][:, :, : RUNS // 2], turned_a[u][:].rearrange("p e (j h) -> p e j h", h=SEG // 2))
-        fold(result[0][:, :, RUNS // 2 :], turned_b[:].rearrange("p e (j h) -> p e j h", h=SEG // 2))
-        nc.sync.dma_start(rows[0], result[0][:])
-        for e in range(2):
-            fold(result[1][:, e, RUNS // 2 :], last[e][:].rearrange("p (j h) -> p j h", h=SEG // 2))
-        nc.sync.dma_start(rows[1], result[1][:])
+            fold(result[:, u, :, RUNS // 2 :], turned_b[u][:].rearrange("p e (j h) -> p e j h", h=SEG // 2))
+            nc.sync.dma_start(rows[u], result[:, u])

@@ -21,7 +21,7 @@ HALF = N // 2
 QHALF = NQ // 2
 RUNS = NQ // SEG
 SCALAR_ROWS = 48
-LATE_SCALAR_ROWS = 88
+LATE_SCALAR_PAIRS = 24
 FLOPS = 2 * N * D * NQ
 
 
@@ -40,7 +40,7 @@ def tile_attend_indexer_topk_kernel(tc, qT, k_words, k_scales, hw, offs, out):
         weights = sb.tile([P, 2, 2], F32, name="weights")
         ident = sb.tile([P, P], F32, name="ident")
         raw_a = sb.tile([P, PACK, QHALF], F32, name="raw_a")
-        grouped = [sb.tile([P, 2, P, PACK], BF16, name="grouped%d" % x, align_bytes=64) for x in range(2)]
+        grouped = [sb.tile([P, 2, P, PACK], BF16, name="grouped%d" % x, tag="grouped%d" % x, align_bytes=64) for x in range(2)]
         q_words = sb.tile([P, NQ], U32, name="q_words", align_bytes=64)
         q_scales = sb.tile([P, NQ], U8, name="q_scales", align_bytes=64)
 
@@ -120,6 +120,8 @@ def tile_attend_indexer_topk_kernel(tc, qT, k_words, k_scales, hw, offs, out):
             return weights[:, c, x : x + 1]
 
         def fresh(kind, x, u, c):
+            if x == 0 and kind == "pooled":
+                return sb.tile([P, HALF], F32, name="pooled_early", tag="grouped1", align_bytes=64)[:]
             if x == 0 and kind in ("first", "pos"):
                 return held[:, 2 * u + c, :]
             return sb.tile([P, HALF], F32, name="%s%d%d%d" % (kind, x, u, c))
@@ -148,8 +150,11 @@ def tile_attend_indexer_topk_kernel(tc, qT, k_words, k_scales, hw, offs, out):
             )
             return total
 
-        def prepare(engine_copy, c, rows):
-            engine_copy(out=grouped[1][:, c, rows], in_=raw_b[:].rearrange("p t (m c) -> p c m t", c=2)[:, c, rows])
+        def prepare(engine_copy, pairs):
+            engine_copy(
+                out=grouped[1][:].rearrange("p c (x i) t -> p x t i c", i=2)[:, pairs],
+                in_=raw_b[:].rearrange("p t (x i c) -> p x t i c", i=2, c=2)[:, pairs],
+            )
 
         def quantise(c):
             cols = slice((2 + c) * P, (3 + c) * P)
@@ -172,9 +177,8 @@ def tile_attend_indexer_topk_kernel(tc, qT, k_words, k_scales, hw, offs, out):
         for u in range(2):
             for c in range(2):
                 acc[0, u, c] = scores(0, u, c)
-        prepare(nc.vector.tensor_copy, 0, slice(0, P))
-        prepare(nc.scalar.copy, 1, slice(0, LATE_SCALAR_ROWS))
-        prepare(nc.vector.tensor_copy, 1, slice(LATE_SCALAR_ROWS, P))
+        prepare(nc.scalar.copy, slice(0, LATE_SCALAR_PAIRS))
+        prepare(nc.vector.tensor_copy, slice(LATE_SCALAR_PAIRS, P // 2))
         quantise(0)
         quantise(1)
         held = sb.tile([P, 4, HALF], F32, name="held", tag="second")

@@ -22,6 +22,7 @@ QHALF = NQ // 2
 RUNS = NQ // SEG
 SCALAR_ROWS = 48
 LATE_SCALAR_PAIRS = 24
+SCALE_ROWS = 16
 FLOPS = 2 * N * D * NQ
 
 
@@ -33,7 +34,8 @@ def tile_attend_indexer_topk_kernel(tc, qT, k_words, k_scales, hw, offs, out):
 
         offsets = sb.tile([P, N // 16], U16, name="offsets")
         pool_words = sb.tile([P, T], I32, name="pool_words", align_bytes=64)
-        pool_scales = sb.tile([P, T], U8, name="pool_scales", align_bytes=64)
+        pool_scales = sb.tile([P, T], U8, name="pool_scales", tag="second", align_bytes=64)
+        spread_scales = sb.tile([P, N], U8, name="spread_scales", align_bytes=64)
         key_words = sb.tile([P, N], U32, name="key_words", align_bytes=64)
         key_scales = sb.tile([P, N], U8, name="key_scales", align_bytes=64)
         weight_rows = sb.tile([P, QHALF], F32, name="weight_rows")
@@ -44,18 +46,22 @@ def tile_attend_indexer_topk_kernel(tc, qT, k_words, k_scales, hw, offs, out):
         q_words = sb.tile([P, NQ], U32, name="q_words", align_bytes=64)
         q_scales = sb.tile([P, NQ], U8, name="q_scales", align_bytes=64)
 
-        nc.vector.memset(pool_scales[:].bitcast(I32), 0)
+        nc.vector.memset(pool_scales[: P - SCALE_ROWS, :].bitcast(I32), 0)
         nc.gpsimd.memset(weight_rows[:], 0.0)
         q_rows = qT[0].rearrange("(p t) q -> p t q", t=PACK)
-        raw_b = sb.tile([P, PACK, QHALF], F32, name="raw_b", tag="second")
-        nc.sync.dma_start(raw_a[:], q_rows[:, :, :QHALF])
+        nc.sync.dma_start(pool_scales[P - SCALE_ROWS :, :].bitcast(I32), k_scales[0].bitcast(I32))
         nc.sync.dma_start(offsets[:], offs)
-        for quad in range(4):
-            nc.sync.dma_start(
-                pool_scales[32 * quad : 32 * quad + 4, :].bitcast(I32), k_scales[0, 4 * quad : 4 * quad + 4].bitcast(I32)
-            )
+        nc.sync.dma_start(raw_a[:], q_rows[:, :, :QHALF])
         nc.sync.dma_start(weight_rows[0:2, :], hw[0].rearrange("o (x q) -> (o x) q", x=2))
         nc.sync.dma_start(pool_words[:], k_words[0].rearrange("p n t -> p (n t)").bitcast(I32))
+        nc.vector.memset(key_scales[:].bitcast(I32), 0)
+        nc.vector.tensor_copy(spread_scales[:], pool_scales[:].indirect(offsets[:]))
+        for quad in range(4):
+            first_row = P - SCALE_ROWS + 4 * quad
+            nc.sync.dma_start(
+                key_scales[32 * quad : 32 * quad + 4, :].bitcast(I32), spread_scales[first_row : first_row + 4, :].bitcast(I32)
+            )
+        raw_b = sb.tile([P, PACK, QHALF], F32, name="raw_b", tag="second", align_bytes=64)
         nc.sync.dma_start(raw_b[:], q_rows[:, :, QHALF:])
 
         zero = sb.tile([P, 1], F32, name="zero")
@@ -67,7 +73,6 @@ def tile_attend_indexer_topk_kernel(tc, qT, k_words, k_scales, hw, offs, out):
         dst = grouped[0][:].rearrange("p c m t -> p m t c")
         nc.scalar.copy(out=dst[:, :SCALAR_ROWS], in_=src[:, :SCALAR_ROWS])
         nc.vector.tensor_copy(out=dst[:, SCALAR_ROWS:], in_=src[:, SCALAR_ROWS:])
-        nc.vector.tensor_copy(key_scales[:], pool_scales[:].indirect(offsets[:]))
         nc.vector.quantize_mx(
             out=q_words[:, :QHALF].bitcast(FP8X4),
             scales=q_scales[:, :QHALF],
@@ -181,7 +186,7 @@ def tile_attend_indexer_topk_kernel(tc, qT, k_words, k_scales, hw, offs, out):
         prepare(nc.vector.tensor_copy, slice(LATE_SCALAR_PAIRS, P // 2))
         quantise(0)
         quantise(1)
-        held = sb.tile([P, 4, HALF], F32, name="held", tag="second")
+        held = sb.tile([P, 4, HALF], F32, name="held", tag="second", align_bytes=64)
         for u in range(2):
             for c in range(2):
                 acc[1, u, c] = scores(1, u, c)

@@ -23,6 +23,7 @@ RUNS = NQ // SEG
 SCALAR_ROWS = 48
 LATE_SCALAR_PAIRS = 24
 SCALE_ROWS = 16
+FREE_ROWS = 1
 FLOPS = 2 * N * D * NQ
 
 
@@ -34,7 +35,7 @@ def tile_attend_indexer_topk_kernel(tc, qT, k_words, k_scales, hw, offs, out):
 
         offsets = sb.tile([P, N // 16], U16, name="offsets")
         pool_words = sb.tile([P, T], I32, name="pool_words", align_bytes=64)
-        pool_scales = sb.tile([P, T], U8, name="pool_scales", tag="second", align_bytes=64)
+        pool_scales = sb.tile([P, T], U8, name="pool_scales", align_bytes=64)
         spread_scales = sb.tile([P, N], U8, name="spread_scales", align_bytes=64)
         key_words = sb.tile([P, N], U32, name="key_words", align_bytes=64)
         key_scales = sb.tile([P, N], U8, name="key_scales", align_bytes=64)
@@ -54,6 +55,8 @@ def tile_attend_indexer_topk_kernel(tc, qT, k_words, k_scales, hw, offs, out):
         nc.sync.dma_start(raw_a[:], q_rows[:, :, :QHALF])
         nc.sync.dma_start(weight_rows[0:2, :], hw[0].rearrange("o (x q) -> (o x) q", x=2))
         nc.sync.dma_start(pool_words[:], k_words[0].rearrange("p n t -> p (n t)").bitcast(I32))
+        raw_b = sb.tile([P, PACK, QHALF], F32, name="raw_b", tag="second", align_bytes=64)
+        nc.sync.dma_start(raw_b[:, :FREE_ROWS], q_rows[:, :FREE_ROWS, QHALF:])
         nc.vector.memset(key_scales[:].bitcast(I32), 0)
         nc.vector.tensor_copy(spread_scales[:], pool_scales[:].indirect(offsets[:]))
         for quad in range(4):
@@ -61,8 +64,7 @@ def tile_attend_indexer_topk_kernel(tc, qT, k_words, k_scales, hw, offs, out):
             nc.sync.dma_start(
                 key_scales[32 * quad : 32 * quad + 4, :].bitcast(I32), spread_scales[first_row : first_row + 4, :].bitcast(I32)
             )
-        raw_b = sb.tile([P, PACK, QHALF], F32, name="raw_b", tag="second", align_bytes=64)
-        nc.sync.dma_start(raw_b[:], q_rows[:, :, QHALF:])
+        nc.sync.dma_start(raw_b[:, FREE_ROWS:], q_rows[:, FREE_ROWS:, QHALF:])
 
         zero = sb.tile([P, 1], F32, name="zero")
         nc.vector.memset(zero[:], 0.0)
@@ -84,16 +86,6 @@ def tile_attend_indexer_topk_kernel(tc, qT, k_words, k_scales, hw, offs, out):
             nc.tensor.transpose(turned_weights[:, c, :], weight_rows[:, c:QHALF:2], ident[:])
         nc.scalar.copy(out=weights[:], in_=turned_weights[:, :, 0:2])
 
-        warm = ps.tile([P, N], F32, name="warm", tag="bank7")
-        nc.tensor.matmul_mx(
-            out=warm[:],
-            lhsT=q_words[:, :P].bitcast(FP8X4),
-            lhsT_scale=q_scales[:, :P],
-            rhs=pool_words[:, :N].bitcast(FP8X4),
-            rhs_scale=key_scales[:],
-            start=True,
-            stop=True,
-        )
         window = pool_words[:].bitcast(U32)
         for u in range(2):
             nc.vector.tensor_copy(

@@ -20,10 +20,11 @@ N, T, D, NQ, SEG = 512, 2048, 512, 512, 16
 HALF = N // 2
 QHALF = NQ // 2
 RUNS = NQ // SEG
-SCALAR_ROWS = 48
-LATE_SCALAR_PAIRS = 24
 SCALE_ROWS = 16
-FREE_ROWS = 1
+FIRST_ROWS = 1
+FREE_ROWS = 2
+CHUNK = 256
+LATE_SCALAR_PAIRS = 24
 FLOPS = 2 * N * D * NQ
 
 
@@ -42,168 +43,211 @@ def tile_attend_indexer_topk_kernel(tc, qT, k_words, k_scales, hw, offs, out):
         weight_rows = sb.tile([P, QHALF], F32, name="weight_rows")
         weights = sb.tile([P, 2, 2], F32, name="weights")
         ident = sb.tile([P, P], F32, name="ident")
-        raw_a = sb.tile([P, PACK, QHALF], F32, name="raw_a")
+        zero = sb.tile([P, 1], F32, name="zero")
+        early_raw = sb.tile([P, PACK, QHALF], F32, name="early_raw")
+        late_raw = sb.tile([P, PACK, QHALF], F32, name="late_raw", tag="late")
         grouped = [sb.tile([P, 2, P, PACK], BF16, name="grouped%d" % x, tag="grouped%d" % x, align_bytes=64) for x in range(2)]
         q_words = sb.tile([P, NQ], U32, name="q_words", align_bytes=64)
         q_scales = sb.tile([P, NQ], U8, name="q_scales", align_bytes=64)
 
         nc.vector.memset(pool_scales[: P - SCALE_ROWS, :].bitcast(I32), 0)
-        nc.gpsimd.memset(weight_rows[:], 0.0)
+        nc.vector.memset(weight_rows[:], 0.0)
+        nc.vector.memset(key_scales[:].bitcast(I32), 0)
+        nc.vector.memset(zero[:], 0.0)
         q_rows = qT[0].rearrange("(p t) q -> p t q", t=PACK)
+        nc.sync.dma_start(early_raw[:, :FIRST_ROWS], q_rows[:, :FIRST_ROWS, :QHALF])
         nc.sync.dma_start(pool_scales[P - SCALE_ROWS :, :].bitcast(I32), k_scales[0].bitcast(I32))
         nc.sync.dma_start(offsets[:], offs)
-        nc.sync.dma_start(raw_a[:], q_rows[:, :, :QHALF])
+        nc.sync.dma_start(early_raw[:, FIRST_ROWS:], q_rows[:, FIRST_ROWS:, :QHALF])
         nc.sync.dma_start(weight_rows[0:2, :], hw[0].rearrange("o (x q) -> (o x) q", x=2))
         nc.sync.dma_start(pool_words[:], k_words[0].rearrange("p n t -> p (n t)").bitcast(I32))
-        raw_b = sb.tile([P, PACK, QHALF], F32, name="raw_b", tag="second", align_bytes=64)
-        nc.sync.dma_start(raw_b[:, :FREE_ROWS], q_rows[:, :FREE_ROWS, QHALF:])
-        nc.vector.memset(key_scales[:].bitcast(I32), 0)
+        nc.sync.dma_start(late_raw[:, :FREE_ROWS], q_rows[:, :FREE_ROWS, QHALF:])
         nc.vector.tensor_copy(spread_scales[:], pool_scales[:].indirect(offsets[:]))
         for quad in range(4):
             first_row = P - SCALE_ROWS + 4 * quad
             nc.sync.dma_start(
                 key_scales[32 * quad : 32 * quad + 4, :].bitcast(I32), spread_scales[first_row : first_row + 4, :].bitcast(I32)
             )
-        nc.sync.dma_start(raw_b[:, FREE_ROWS:], q_rows[:, FREE_ROWS:, QHALF:])
+        nc.sync.dma_start(late_raw[:, FREE_ROWS:], q_rows[:, FREE_ROWS:, QHALF:])
 
-        zero = sb.tile([P, 1], F32, name="zero")
-        nc.vector.memset(zero[:], 0.0)
         nc.scalar.copy(out=ident[:], in_=zero[:].to_broadcast([P, P]))
         make_identity(nc, ident[:], nomemset=True)
 
-        src = raw_a[:].rearrange("p t (m c) -> p m t c", c=2)
-        dst = grouped[0][:].rearrange("p c m t -> p m t c")
-        nc.scalar.copy(out=dst[:, :SCALAR_ROWS], in_=src[:, :SCALAR_ROWS])
-        nc.vector.tensor_copy(out=dst[:, SCALAR_ROWS:], in_=src[:, SCALAR_ROWS:])
-        nc.vector.quantize_mx(
-            out=q_words[:, :QHALF].bitcast(FP8X4),
-            scales=q_scales[:, :QHALF],
-            in_=grouped[0][:].rearrange("p c m t -> p (c m t)"),
-        )
+        def cast_group(c):
+            nc.scalar.copy(
+                out=grouped[0][:, c].rearrange("p (m i) t -> p m t i", i=2),
+                in_=early_raw[:].rearrange("p t (m i c) -> p c m t i", i=2, c=2)[:, c],
+            )
+
+        def cast_late(engine_copy, pairs):
+            engine_copy(
+                out=grouped[1][:].rearrange("p c (x i) t -> p x t i c", i=2)[:, pairs],
+                in_=late_raw[:].rearrange("p t (x i c) -> p x t i c", i=2, c=2)[:, pairs],
+            )
+
+        def quantise(x, c):
+            cols = slice((2 * x + c) * P, (2 * x + c + 1) * P)
+            nc.vector.quantize_mx(
+                out=q_words[:, cols].bitcast(FP8X4),
+                scales=q_scales[:, cols],
+                in_=grouped[x][:, c].rearrange("p m t -> p (m t)"),
+            )
+
+        for c in range(2):
+            cast_group(c)
+            quantise(0, c)
 
         turned_weights = ps.tile([P, 2, P], F32, name="turned_weights", tag="bank7")
         for c in range(2):
             nc.tensor.transpose(turned_weights[:, c, :], weight_rows[:, c:QHALF:2], ident[:])
         nc.scalar.copy(out=weights[:], in_=turned_weights[:, :, 0:2])
+        spread_weights = ps.tile([P, 2, P], F32, name="spread_weights", tag="bank6")
+        for c in range(2):
+            nc.tensor.transpose(spread_weights[:, c, :], weights[:, c, 1:2].to_broadcast([P, P]), ident[:])
+        weight_row = sb.tile([P, 2, P], F32, name="weight_row")
+        nc.scalar.copy(out=weight_row[:], in_=spread_weights[:])
 
-        window = pool_words[:].bitcast(U32)
-        for u in range(2):
-            nc.vector.tensor_copy(
-                key_words[:, u * HALF : (u + 1) * HALF],
-                window.indirect(offsets[:, u * HALF // 16 : (u + 1) * HALF // 16]),
-            )
+        warm = ps.tile([P, 256], F32, name="warm", tag="bank6")
+        nc.tensor.matmul_mx(
+            out=warm[:],
+            lhsT=q_words[:, :P].bitcast(FP8X4),
+            lhsT_scale=q_scales[:, :P],
+            rhs=q_words[:, :256].bitcast(FP8X4),
+            rhs_scale=q_scales[:, :256],
+            start=True,
+            stop=True,
+        )
 
-        def scores(x, u, c):
-            acc = ps.tile([P, HALF], F32, name="acc%d%d%d" % (x, u, c), tag="bank%d" % (4 * x + 2 * u + c))
+        acc = {}
+        for x in range(2):
+            for u in range(2):
+                for c in range(2):
+                    acc[x, u, c] = ps.tile([P, HALF], F32, name="acc%d%d%d" % (x, u, c), tag="bank%d" % (4 * x + 2 * u + c))
+
+        def scores(x, c, first_slot, width):
             cols = slice((2 * x + c) * P, (2 * x + c + 1) * P)
+            slots = slice(first_slot, first_slot + width)
             nc.tensor.matmul_mx(
-                out=acc[:],
+                out=acc[x, first_slot // HALF, c][:, first_slot % HALF : first_slot % HALF + width],
                 lhsT=q_words[:, cols].bitcast(FP8X4),
                 lhsT_scale=q_scales[:, cols],
-                rhs=key_words[:, u * HALF : (u + 1) * HALF].bitcast(FP8X4),
-                rhs_scale=key_scales[:, u * HALF : (u + 1) * HALF],
+                rhs=key_words[:, slots].bitcast(FP8X4),
+                rhs_scale=key_scales[:, slots],
                 start=True,
                 stop=True,
             )
-            return acc
 
-        def by_parity(tile):
-            return tile[:].rearrange("p (s e) -> p e s", e=2)
+        window = pool_words[:].bitcast(U32)
+        for first_slot in range(0, N, CHUNK):
+            nc.vector.tensor_copy(
+                key_words[:, first_slot : first_slot + CHUNK],
+                window.indirect(offsets[:, first_slot // 16 : (first_slot + CHUNK) // 16]),
+            )
+            for c in range(2):
+                scores(0, c, first_slot, CHUNK)
 
-        def parted(tile):
-            return tile[:].rearrange("p (e s) -> p e s", e=2)
+        def by_block(x, u, c):
+            return acc[x, u, c][:].rearrange("p (e s) -> p e s" if u else "p (s e) -> p e s", e=2)
+
+        def parted(part):
+            return part.rearrange("p (e s) -> p e s", e=2)
 
         def weight(x, c):
             return weights[:, c, x : x + 1]
 
         def fresh(kind, x, u, c):
-            if x == 0 and kind == "pooled":
-                return sb.tile([P, HALF], F32, name="pooled_early", tag="grouped1", align_bytes=64)[:]
-            if x == 0 and kind in ("first", "pos"):
-                return held[:, 2 * u + c, :]
-            return sb.tile([P, HALF], F32, name="%s%d%d%d" % (kind, x, u, c))
+            return sb.tile([P, HALF], F32, name="%s%d%d%d" % (kind, x, u, c))[:]
 
-        def first(x, u, c):
-            total = fresh("first", x, u, c)
+        def weighed(part, x, u, c):
             nc.vector.tensor_scalar(
-                out=parted(total), in0=by_parity(acc[x, u, c]), scalar1=0.0, scalar2=weight(x, c), op0=ALU.max, op1=ALU.mult
+                out=parted(part), in0=by_block(x, u, c), scalar1=0.0, scalar2=weight(x, c), op0=ALU.max, op1=ALU.mult
             )
-            return total
+            return part
 
-        def relu(x, u, c):
-            pos = fresh("pos", x, u, c)
-            nc.scalar.activation(parted(pos), by_parity(acc[x, u, c]), ACT.Relu)
+        def relu(pos, x, u, c):
+            nc.scalar.activation(parted(pos), by_block(x, u, c), ACT.Relu)
             return pos
 
-        def scaled(x, u, c, pos):
-            total = fresh("scaled", x, u, c)
-            nc.scalar.activation(total[:], pos[:], ACT.Copy, scale=weight(x, c))
-            return total
+        def scaled(part, pos, x, c):
+            nc.scalar.activation(part, pos, ACT.Copy, scale=weight(x, c))
+            return part
 
-        def pooled(x, u, c, pos):
-            total = fresh("pooled", x, u, c)
-            nc.gpsimd.tensor_scalar(
-                out=total[:], in0=pos[:], scalar1=weight(x, c), scalar2=zero[:], op0=ALU.mult, op1=ALU.add
-            )
-            return total
-
-        def prepare(engine_copy, pairs):
-            engine_copy(
-                out=grouped[1][:].rearrange("p c (x i) t -> p x t i c", i=2)[:, pairs],
-                in_=raw_b[:].rearrange("p t (x i c) -> p x t i c", i=2, c=2)[:, pairs],
-            )
-
-        def quantise(c):
-            cols = slice((2 + c) * P, (3 + c) * P)
-            nc.vector.quantize_mx(
-                out=q_words[:, cols].bitcast(FP8X4),
-                scales=q_scales[:, cols],
-                in_=grouped[1][:, c].rearrange("p m t -> p (m t)"),
-            )
+        def pooled(part, pos, x, c):
+            nc.gpsimd.tensor_scalar(out=part, in0=pos, scalar1=weight(x, c), scalar2=0.0, op0=ALU.mult, op1=ALU.add)
+            return part
 
         def turn(bank, part, e, start, stop):
             nc.tensor.matmul(bank, part[:, e * P : (e + 1) * P], ident[:], start=start, stop=stop, is_transpose=True)
 
         result = sb.tile([P, 2, 2, RUNS], F32, name="result")
-        rows = out[0].rearrange("(u p e) j -> u p e j", p=P, e=2)
 
         def fold(dest, bank):
             nc.vector.tensor_reduce(out=dest, in_=bank, axis=AX.X, op=ALU.add)
 
-        acc = {}
-        for u in range(2):
-            for c in range(2):
-                acc[0, u, c] = scores(0, u, c)
-        prepare(nc.scalar.copy, slice(0, LATE_SCALAR_PAIRS))
-        prepare(nc.vector.tensor_copy, slice(LATE_SCALAR_PAIRS, P // 2))
-        quantise(0)
-        quantise(1)
-        held = sb.tile([P, 4, HALF], F32, name="held", tag="second", align_bytes=64)
-        for u in range(2):
-            for c in range(2):
-                acc[1, u, c] = scores(1, u, c)
-        pos_a00 = relu(0, 0, 0)
-        pos_a10 = relu(0, 1, 0)
-        a01 = first(0, 0, 1)
-        a11 = first(0, 1, 1)
-        a00 = pooled(0, 0, 0, pos_a00)
-        a10 = scaled(0, 1, 0, pos_a10)
-        pos_b00 = relu(1, 0, 0)
-        b00 = pooled(1, 0, 0, pos_b00)
-        b01 = first(1, 0, 1)
-        pos_b10 = relu(1, 1, 0)
-        b10 = scaled(1, 1, 0, pos_b10)
-        b11 = first(1, 1, 1)
+        def slot_scores(b):
+            slots = slice(HALF + b * P, HALF + (b + 1) * P)
+            nc.tensor.matmul_mx(
+                out=acc[1, 1, b][:],
+                lhsT=key_words[:, slots].bitcast(FP8X4),
+                lhsT_scale=key_scales[:, slots],
+                rhs=q_words[:, QHALF:].bitcast(FP8X4),
+                rhs_scale=q_scales[:, QHALF:],
+                start=True,
+                stop=True,
+            )
+
+        def slot_products(b):
+            products = fresh("products", 1, 1, b)
+            nc.vector.scalar_tensor_tensor(
+                out=products,
+                in0=acc[1, 1, b][:],
+                scalar=0.0,
+                in1=weight_row[:].rearrange("p c m -> p (c m)"),
+                op0=ALU.max,
+                op1=ALU.mult,
+            )
+            return products
+
+        def slot_fold(b, products):
+            nc.vector.tensor_reduce(
+                out=result[:, 1, b, RUNS // 2 :],
+                in_=products.rearrange("p (c j h) -> p j c h", c=2, h=SEG // 2),
+                axis=AX.XY,
+                op=ALU.add,
+            )
+
+        cast_late(nc.scalar.copy, slice(0, LATE_SCALAR_PAIRS))
+        cast_late(nc.vector.tensor_copy, slice(LATE_SCALAR_PAIRS, P // 2))
+        quantise(1, 0)
+        quantise(1, 1)
+        scores(1, 0, 0, HALF)
+        scores(1, 1, 0, HALF)
+        slot_scores(0)
+        slot_scores(1)
+        held = sb.tile([P, 4, HALF], F32, name="held", tag="late")
+        pos_a00 = relu(held[:, 0], 0, 0, 0)
+        pos_a10 = relu(held[:, 2], 0, 1, 0)
+        a01 = weighed(held[:, 1], 0, 0, 1)
+        a11 = weighed(held[:, 3], 0, 1, 1)
+        after_quantise = sb.tile([P, HALF], F32, name="after_quantise", tag="grouped1", align_bytes=64)
+        a10 = pooled(after_quantise[:], pos_a10, 0, 0)
+        a00 = scaled(fresh("scaled", 0, 0, 0), pos_a00, 0, 0)
+        pos_b00 = relu(fresh("pos", 1, 0, 0), 1, 0, 0)
+        b00 = pooled(fresh("pooled", 1, 0, 0), pos_b00, 1, 0)
+        pos_b01 = relu(fresh("pos", 1, 0, 1), 1, 0, 1)
+        b01 = scaled(fresh("scaled", 1, 0, 1), pos_b01, 1, 1)
+        products = [slot_products(b) for b in range(2)]
         turned_a = ps.tile([P, 2, 2, P], F32, name="turned_a", tag="bank0")
-        for u, part in ((0, a01), (1, a11), (0, a00), (1, a10)):
+        for u, part in ((0, a01), (0, a00), (1, a11), (1, a10)):
             for e in range(2):
                 turn(turned_a[:, u, e, :], part, e, part is a01 and e == 0, part is a10 and e == 1)
-        turned_b = [ps.tile([P, 2, P], F32, name="turned_b%d" % u, tag="bank%d" % (1 + u)) for u in range(2)]
-        for u, parts in enumerate(((b01, b00), (b11, b10))):
-            for part in parts:
-                for e in range(2):
-                    turn(turned_b[u][:, e, :], part, e, part is parts[0] and e == 0, part is parts[1] and e == 1)
+        turned_b = ps.tile([P, 2, P], F32, name="turned_b", tag="bank1")
+        for part in (b00, b01):
+            for e in range(2):
+                turn(turned_b[:, e, :], part, e, part is b00 and e == 0, part is b01 and e == 1)
+        slot_fold(0, products[0])
+        slot_fold(1, products[1])
         fold(result[:, :, :, : RUNS // 2], turned_a[:].rearrange("p u e (j h) -> p u e j h", h=SEG // 2))
-        for u in range(2):
-            fold(result[:, u, :, RUNS // 2 :], turned_b[u][:].rearrange("p e (j h) -> p e j h", h=SEG // 2))
-            nc.sync.dma_start(rows[u], result[:, u])
+        nc.sync.dma_start(out[0, HALF:].rearrange("(b p) j -> p b j", p=P), result[:, 1])
+        fold(result[:, 0, :, RUNS // 2 :], turned_b[:].rearrange("p e (j h) -> p e j h", h=SEG // 2))
+        nc.sync.dma_start(out[0, :HALF].rearrange("(p e) j -> p e j", e=2), result[:, 0])

@@ -107,17 +107,6 @@ def tile_attend_indexer_topk_kernel(tc, qT, k_words, k_scales, hw, offs, out):
         weight_row = sb.tile([P, 2, P], F32, name="weight_row")
         nc.scalar.copy(out=weight_row[:], in_=spread_weights[:])
 
-        warm = ps.tile([P, 256], F32, name="warm", tag="bank6")
-        nc.tensor.matmul_mx(
-            out=warm[:],
-            lhsT=q_words[:, :P].bitcast(FP8X4),
-            lhsT_scale=q_scales[:, :P],
-            rhs=q_words[:, :256].bitcast(FP8X4),
-            rhs_scale=q_scales[:, :256],
-            start=True,
-            stop=True,
-        )
-
         acc = {}
         for x in range(2):
             for u in range(2):

@@ -56,7 +56,7 @@ def tile_attend_indexer_topk_kernel(tc, qT, k_words, k_scales, hw, offs, out):
         nc.vector.memset(zero[:], 0.0)
         q_rows = qT[0].rearrange("(p t) q -> p t q", t=PACK)
         nc.sync.dma_start(early_raw[:, :FIRST_ROWS], q_rows[:, :FIRST_ROWS, :QHALF])
-        nc.sync.dma_start(pool_scales[P - SCALE_ROWS :, :].bitcast(I32), k_scales[0].bitcast(I32))
+        nc.scalar.dma_start(pool_scales[P - SCALE_ROWS :, :].bitcast(I32), k_scales[0].bitcast(I32))
         nc.sync.dma_start(offsets[:], offs)
         nc.sync.dma_start(early_raw[:, FIRST_ROWS:], q_rows[:, FIRST_ROWS:, :QHALF])
         nc.sync.dma_start(weight_rows[0:2, :], hw[0].rearrange("o (x q) -> (o x) q", x=2))

from contextlib import ExitStack

import concourse.mybir as mybir
from concourse.masks import make_identity

F32 = mybir.dt.float32
BF16 = mybir.dt.bfloat16
I32 = mybir.dt.int32
U32 = mybir.dt.uint32
U16 = mybir.dt.uint16
U8 = mybir.dt.uint8
FP8X4 = mybir.dt.float8_e4m3fn_x4
ALU = mybir.AluOpType
AX = mybir.AxisListType
ACT = mybir.ActivationFunctionType

P = 128
PACK = 4
N, T, D, NQ, SEG = 512, 2048, 512, 512, 16
HALF = N // 2
QHALF = NQ // 2
RUNS = NQ // SEG
SCALE_ROWS = 16
FIRST_ROWS = 1
FREE_ROWS = 2
CHUNK = 256
LATE_SCALAR_PAIRS = 24
FLOPS = 2 * N * D * NQ


def tile_attend_indexer_topk_kernel(tc, qT, k_words, k_scales, hw, offs, out):
    nc = tc.nc
    with ExitStack() as ctx:
        sb = ctx.enter_context(tc.tile_pool(name="sb", bufs=1))
        ps = ctx.enter_context(tc.psum_pool(name="ps", bufs=1))

        offsets = sb.tile([P, N // 16], U16, name="offsets")
        pool_words = sb.tile([P, T], I32, name="pool_words", align_bytes=64)
        pool_scales = sb.tile([P, T], U8, name="pool_scales", align_bytes=64)
        spread_scales = sb.tile([P, N], U8, name="spread_scales", align_bytes=64)
        key_words = sb.tile([P, N], U32, name="key_words", align_bytes=64)
        key_scales = sb.tile([P, N], U8, name="key_scales", align_bytes=64)
        weight_rows = sb.tile([P, QHALF], F32, name="weight_rows")
        weights = sb.tile([P, 2, 2], F32, name="weights")
        ident = sb.tile([P, P], F32, name="ident")
        zero = sb.tile([P, 1], F32, name="zero")
        early_raw = sb.tile([P, PACK, QHALF], F32, name="early_raw")
        late_raw = sb.tile([P, PACK, QHALF], F32, name="late_raw", tag="late")
        grouped = [sb.tile([P, 2, P, PACK], BF16, name="grouped%d" % x, tag="grouped%d" % x, align_bytes=64) for x in range(2)]
        q_words = sb.tile([P, NQ], U32, name="q_words", align_bytes=64)
        q_scales = sb.tile([P, NQ], U8, name="q_scales", align_bytes=64)

        nc.vector.memset(pool_scales[: P - SCALE_ROWS, :].bitcast(I32), 0)
        nc.vector.memset(weight_rows[:], 0.0)
        nc.vector.memset(key_scales[:].bitcast(I32), 0)
        nc.vector.memset(zero[:], 0.0)
        q_rows = qT[0].rearrange("(p t) q -> p t q", t=PACK)
        nc.sync.dma_start(early_raw[:, :FIRST_ROWS], q_rows[:, :FIRST_ROWS, :QHALF])
        nc.scalar.dma_start(pool_scales[P - SCALE_ROWS :, :].bitcast(I32), k_scales[0].bitcast(I32))
        nc.sync.dma_start(offsets[:], offs)
        nc.sync.dma_start(early_raw[:, FIRST_ROWS:], q_rows[:, FIRST_ROWS:, :QHALF])
        nc.sync.dma_start(weight_rows[0:2, :], hw[0].rearrange("o (x q) -> (o x) q", x=2))
        nc.sync.dma_start(pool_words[:], k_words[0].rearrange("p n t -> p (n t)").bitcast(I32))
        nc.sync.dma_start(late_raw[:, :FREE_ROWS], q_rows[:, :FREE_ROWS, QHALF:])
        nc.vector.tensor_copy(spread_scales[:], pool_scales[:].indirect(offsets[:]))
        for quad in range(4):
            first_row = P - SCALE_ROWS + 4 * quad
            nc.sync.dma_start(
                key_scales[32 * quad : 32 * quad + 4, :].bitcast(I32), spread_scales[first_row : first_row + 4, :].bitcast(I32)
            )
        nc.sync.dma_start(late_raw[:, FREE_ROWS:], q_rows[:, FREE_ROWS:, QHALF:])

        nc.scalar.copy(out=ident[:], in_=zero[:].to_broadcast([P, P]))
        make_identity(nc, ident[:], nomemset=True)

        def cast_group(c):
            nc.scalar.copy(
                out=grouped[0][:, c].rearrange("p (m i) t -> p m t i", i=2),
                in_=early_raw[:].rearrange("p t (m i c) -> p c m t i", i=2, c=2)[:, c],
            )

        def cast_late(engine_copy, pairs):
            engine_copy(
                out=grouped[1][:].rearrange("p c (x i) t -> p x t i c", i=2)[:, pairs],
                in_=late_raw[:].rearrange("p t (x i c) -> p x t i c", i=2, c=2)[:, pairs],
            )

        def quantise(x, c):
            cols = slice((2 * x + c) * P, (2 * x + c + 1) * P)
            nc.vector.quantize_mx(
                out=q_words[:, cols].bitcast(FP8X4),
                scales=q_scales[:, cols],
                in_=grouped[x][:, c].rearrange("p m t -> p (m t)"),
            )

        for c in range(2):
            cast_group(c)
            quantise(0, c)

        turned_weights = ps.tile([P, 2, P], F32, name="turned_weights", tag="bank7")
        for c in range(2):
            nc.tensor.transpose(turned_weights[:, c, :], weight_rows[:, c:QHALF:2], ident[:])
        nc.scalar.copy(out=weights[:], in_=turned_weights[:, :, 0:2])
        spread_weights = ps.tile([P, 2, P], F32, name="spread_weights", tag="bank6")
        for c in range(2):
            nc.tensor.transpose(spread_weights[:, c, :], weights[:, c, 1:2].to_broadcast([P, P]), ident[:])
        weight_row = sb.tile([P, 2, P], F32, name="weight_row")
        nc.scalar.copy(out=weight_row[:], in_=spread_weights[:])

        acc = {}
        for x in range(2):
            for u in range(2):
                for c in range(2):
                    acc[x, u, c] = ps.tile([P, HALF], F32, name="acc%d%d%d" % (x, u, c), tag="bank%d" % (4 * x + 2 * u + c))

        def scores(x, c, first_slot, width):
            cols = slice((2 * x + c) * P, (2 * x + c + 1) * P)
            slots = slice(first_slot, first_slot + width)
            nc.tensor.matmul_mx(
                out=acc[x, first_slot // HALF, c][:, first_slot % HALF : first_slot % HALF + width],
                lhsT=q_words[:, cols].bitcast(FP8X4),
                lhsT_scale=q_scales[:, cols],
                rhs=key_words[:, slots].bitcast(FP8X4),
                rhs_scale=key_scales[:, slots],
                start=True,
                stop=True,
            )

        window = pool_words[:].bitcast(U32)
        for first_slot in range(0, N, CHUNK):
            nc.vector.tensor_copy(
                key_words[:, first_slot : first_slot + CHUNK],
                window.indirect(offsets[:, first_slot // 16 : (first_slot + CHUNK) // 16]),
            )
            for c in range(2):
                scores(0, c, first_slot, CHUNK)

        def by_block(x, u, c):
            return acc[x, u, c][:].rearrange("p (e s) -> p e s" if u else "p (s e) -> p e s", e=2)

        def parted(part):
            return part.rearrange("p (e s) -> p e s", e=2)

        def weight(x, c):
            return weights[:, c, x : x + 1]

        def fresh(kind, x, u, c):
            return sb.tile([P, HALF], F32, name="%s%d%d%d" % (kind, x, u, c))[:]

        def weighed(part, x, u, c):
            nc.vector.tensor_scalar(
                out=parted(part), in0=by_block(x, u, c), scalar1=0.0, scalar2=weight(x, c), op0=ALU.max, op1=ALU.mult
            )
            return part

        def relu(pos, x, u, c):
            nc.scalar.activation(parted(pos), by_block(x, u, c), ACT.Relu)
            return pos

        def scaled(part, pos, x, c):
            nc.scalar.activation(part, pos, ACT.Copy, scale=weight(x, c))
            return part

        def pooled(part, pos, x, c):
            nc.gpsimd.tensor_scalar(out=part, in0=pos, scalar1=weight(x, c), scalar2=0.0, op0=ALU.mult, op1=ALU.add)
            return part

        def turn(bank, part, e, start, stop):
            nc.tensor.matmul(bank, part[:, e * P : (e + 1) * P], ident[:], start=start, stop=stop, is_transpose=True)

        result = sb.tile([P, 2, 2, RUNS], F32, name="result")

        def fold(dest, bank):
            nc.vector.tensor_reduce(out=dest, in_=bank, axis=AX.X, op=ALU.add)

        def slot_scores(b):
            slots = slice(HALF + b * P, HALF + (b + 1) * P)
            nc.tensor.matmul_mx(
                out=acc[1, 1, b][:],
                lhsT=key_words[:, slots].bitcast(FP8X4),
                lhsT_scale=key_scales[:, slots],
                rhs=q_words[:, QHALF:].bitcast(FP8X4),
                rhs_scale=q_scales[:, QHALF:],
                start=True,
                stop=True,
            )

        def slot_products(b):
            products = fresh("products", 1, 1, b)
            nc.vector.scalar_tensor_tensor(
                out=products,
                in0=acc[1, 1, b][:],
                scalar=0.0,
                in1=weight_row[:].rearrange("p c m -> p (c m)"),
                op0=ALU.max,
                op1=ALU.mult,
            )
            return products

        def slot_fold(b, products):
            nc.vector.tensor_reduce(
                out=result[:, 1, b, RUNS // 2 :],
                in_=products.rearrange("p (c j h) -> p j c h", c=2, h=SEG // 2),
                axis=AX.XY,
                op=ALU.add,
            )

        cast_late(nc.scalar.copy, slice(0, LATE_SCALAR_PAIRS))
        cast_late(nc.vector.tensor_copy, slice(LATE_SCALAR_PAIRS, P // 2))
        quantise(1, 0)
        quantise(1, 1)
        scores(1, 0, 0, HALF)
        scores(1, 1, 0, HALF)
        slot_scores(0)
        slot_scores(1)
        held = sb.tile([P, 4, HALF], F32, name="held", tag="late")
        pos_a00 = relu(held[:, 0], 0, 0, 0)
        pos_a10 = relu(held[:, 2], 0, 1, 0)
        a01 = weighed(held[:, 1], 0, 0, 1)
        a11 = weighed(held[:, 3], 0, 1, 1)
        after_quantise = sb.tile([P, HALF], F32, name="after_quantise", tag="grouped1", align_bytes=64)
        a10 = pooled(after_quantise[:], pos_a10, 0, 0)
        a00 = scaled(fresh("scaled", 0, 0, 0), pos_a00, 0, 0)
        pos_b00 = relu(fresh("pos", 1, 0, 0), 1, 0, 0)
        b00 = pooled(fresh("pooled", 1, 0, 0), pos_b00, 1, 0)
        pos_b01 = relu(fresh("pos", 1, 0, 1), 1, 0, 1)
        b01 = scaled(fresh("scaled", 1, 0, 1), pos_b01, 1, 1)
        products = [slot_products(b) for b in range(2)]
        turned_a = ps.tile([P, 2, 2, P], F32, name="turned_a", tag="bank0")
        for u, part in ((0, a01), (0, a00), (1, a11), (1, a10)):
            for e in range(2):
                turn(turned_a[:, u, e, :], part, e, part is a01 and e == 0, part is a10 and e == 1)
        turned_b = ps.tile([P, 2, P], F32, name="turned_b", tag="bank1")
        for part in (b00, b01):
            for e in range(2):
                turn(turned_b[:, e, :], part, e, part is b00 and e == 0, part is b01 and e == 1)
        slot_fold(0, products[0])
        slot_fold(1, products[1])
        fold(result[:, :, :, : RUNS // 2], turned_a[:].rearrange("p u e (j h) -> p u e j h", h=SEG // 2))
        nc.sync.dma_start(out[0, HALF:].rearrange("(b p) j -> p b j", p=P), result[:, 1])
        fold(result[:, 0, :, RUNS // 2 :], turned_b[:].rearrange("p e (j h) -> p e j h", h=SEG // 2))
        nc.sync.dma_start(out[0, :HALF].rearrange("(p e) j -> p e j", e=2), result[:, 0])
